import numpy as np
import ml_dtypes


def mxq(x, axis, fmt="e4m3"):
    dtype, down = {"e4m3": (ml_dtypes.float8_e4m3fn, 7), "e5m2": (ml_dtypes.float8_e5m2, 14)}[fmt]
    v = np.moveaxis(np.asarray(x, np.float32).astype(ml_dtypes.bfloat16).astype(np.float64), axis, -1)
    blocks = v.reshape(v.shape[:-1] + (-1, 32))
    amax = np.abs(blocks).max(-1, keepdims=True)
    byte = np.maximum(np.where(amax > 0, np.frexp(amax)[1] - 1 + 127, 0) - down, 1)
    scale = np.exp2(byte - 127.0)
    codes = (blocks / scale).astype(np.float32).astype(dtype).astype(np.float64)
    return np.moveaxis((codes * scale).reshape(v.shape), -1, axis)


WIDE = False


def mx_kscale(k):
    if not WIDE:
        return np.ones(k)
    levels = np.array([10, -10, 5, -5, 0])
    if k % 512:
        return np.exp2(np.random.permutation(np.resize(levels, k // 32))).repeat(32)
    a = np.empty((k // 512, 16))
    for p in range(k // 512):
        a[p, :8] = np.random.permutation(np.resize(levels, 8))
        for g in range(8):
            far = levels[np.abs(levels - a[p, g]) >= 10]
            a[p, g + 8] = far[np.random.randint(len(far))]
    return np.exp2(a.ravel()).repeat(32)


BF16 = ml_dtypes.bfloat16


def bf(x):
    return np.asarray(x, np.float32).astype(BF16)


def f64(x):
    return np.asarray(x).astype(np.float64)


E2M1 = np.array([0.0, 0.5, 1.0, 1.5, 2.0, 3.0, 4.0, 6.0, -0.0, -0.5, -1.0, -1.5, -2.0, -3.0, -4.0, -6.0])


def pack_weight(w, fmt):
    k, n = w.shape
    w = f64(bf(w)).reshape(k // 32, 32, n)
    amax = np.abs(w).max(1)
    if fmt == "e4m3":
        byte = np.frexp(amax)[1] - 1 + 127 - 7
    else:
        mant, ex = np.frexp(amax / 6.0)
        byte = np.where(mant > 0.5, ex, ex - 1) + 127
    byte = np.clip(np.where(amax > 0, byte, 1), 1, 254)
    scaled = (w * np.exp2(127.0 - byte)[:, None, :]).reshape(k, n).astype(np.float32)
    by_word = np.ascontiguousarray(scaled.reshape(k // 512, 128, 4, n).transpose(0, 1, 3, 2))
    if fmt == "e4m3":
        words = by_word.astype(ml_dtypes.float8_e4m3fn).view(np.uint8)
    else:
        c = by_word.astype(ml_dtypes.float4_e2m1fn).view(np.uint8) & 0xF
        words = c[..., 0::2] | (c[..., 1::2] << 4)
    return np.ascontiguousarray(words), np.ascontiguousarray(byte.astype(np.uint8).reshape(k // 512, 16, n))


def unpack_weight(words, scales, fmt):
    g, p, n, _ = words.shape
    if fmt == "e4m3":
        vals = np.ascontiguousarray(words).view(ml_dtypes.float8_e4m3fn).astype(np.float64)
    else:
        nib = np.empty((g, p, n, 4), np.uint8)
        nib[..., 0::2] = words & 0xF
        nib[..., 1::2] = words >> 4
        vals = E2M1[nib]
    vals = vals * np.repeat(np.exp2(scales.astype(np.float64) - 127.0), 8, axis=1)[..., None]
    return vals.transpose(0, 1, 3, 2).reshape(g * 512, n)
def pack4(w):
    words, scales = pack_weight(w, "e2m1")
    return words.reshape(words.shape[0], 128, -1), scales


def unpack4(words, scales):
    return unpack_weight(words.reshape(words.shape[0], 128, -1, 2), scales, "e2m1")


def planes(Y):
    n, m = Y.shape
    b = f64(bf(Y)).reshape(n // 32, 32, m)
    amax = np.abs(b).max(1)
    byte = np.clip(np.where(amax > 0, np.frexp(amax)[1] - 1 + 127 - 7, 1), 1, 254)
    codes = (b * np.exp2(127.0 - byte)[:, None, :]).reshape(n, m).astype(np.float32).astype(ml_dtypes.float8_e4m3fn).view(np.uint8)
    words = codes.reshape(n // 512, 128, 4, m).transpose(0, 1, 3, 2)
    return np.ascontiguousarray(words), np.ascontiguousarray(byte.astype(np.uint8).reshape(n // 512, 16, m))


B, N, M, D = 2, 1024, 768, 512


def log_sigmoid(t):
    return -(np.maximum(-t, 0.0) + np.log1p(np.exp(-np.abs(t))))


def log_normalise(s, axis):
    m = s.max(axis=axis, keepdims=True)
    return s - (m + np.log(np.sum(np.exp(s - m), axis=axis, keepdims=True)))


def setup_inputs():
    s, t = mx_kscale(D), mx_kscale(D)
    ga = 0.6 + 0.8 * np.random.random((B, N, 1))
    gb = 0.6 + 0.8 * np.random.random((B, M, 1))
    xa = bf(np.random.standard_normal((B, N, D)) * ga * s)
    xb = bf(np.random.standard_normal((B, M, D)) * gb / t)
    w_words, w_scales = pack4(np.random.standard_normal((D, D)) / np.sqrt(D) / s[:, None] * t)
    return {
        "xa": xa,
        "xb": xb,
        "w_words": w_words,
        "w_scales": w_scales,
        "b": bf(np.random.standard_normal(D) * 0.3 * t),
        "wza": bf(np.random.standard_normal(D) / np.sqrt(D) / s),
        "wzb": bf(np.random.standard_normal(D) / np.sqrt(D) * t),
    }


def core(xa, xb, w_words, w_scales, b, wza, wzb):
    xa, xb = f64(xa), f64(xb)

    q = (mxq(xa, 2, "e4m3") @ unpack4(w_words, w_scales)) + f64(b)
    s = (mxq(q, 2, "e4m3") @ mxq(xb, 2, "e4m3").transpose(0, 2, 1)) / np.sqrt(D)

    lr = log_normalise(s, 2)
    lc = log_normalise(s, 1)

    za = np.sum(xa * f64(wza), axis=-1)
    zb = np.sum(xb * f64(wzb), axis=-1)

    y = lr + lc + log_sigmoid(za)[:, :, None] + log_sigmoid(zb)[:, None, :]
    return y + np.log(N) + np.log(M)


def reference(xa, xb, w_words, w_scales, b, wza, wzb):
    R_out = core(xa, xb, w_words, w_scales, b, wza, wzb)
    words, scales = planes(np.moveaxis(R_out, 1, 0).reshape(1024, -1))
    return R_out, words, scales

@@ -1,0 +1,569 @@
+import math
+from contextlib import ExitStack
+
+import concourse.mybir as mybir
+from concourse.masks import make_identity
+
+B, N, M, D = 2, 1024, 768, 512
+FLOPS = 2 * B * N * D * D + 2 * B * N * M * D
+
+F32 = mybir.dt.float32
+BF16 = mybir.dt.bfloat16
+U32 = mybir.dt.uint32
+I32 = mybir.dt.int32
+U8 = mybir.dt.uint8
+FP8X4 = mybir.dt.float8_e4m3fn_x4
+FP4X4 = mybir.dt.float4_e2m1fn_x4
+ALU = mybir.AluOpType
+ACT = mybir.ActivationFunctionType
+AXIS = mybir.AxisListType
+
+P = 128
+PACK = 4
+BANK = 512
+GROUPS = N // (P * PACK)
+M_TILES = M // P
+STATS = M_TILES + GROUPS * PACK
+C = 1.0 / math.sqrt(D)
+HALF_CONST = 0.5 * (math.log(N) + math.log(M))
+ROOT = 512.0
+
+
+def tile_lightgluematchabilityassignment_x2_kernel(
+    tc, xa, xb, w_words, w_scales, b, wza, wzb, out_0, out_1, out_2
+):
+    nc = tc.nc
+    with ExitStack() as ctx:
+        keep = ctx.enter_context(tc.tile_pool(name="keep", bufs=1))
+        rot = ctx.enter_context(tc.tile_pool(name="rot", bufs=2))
+        psum = ctx.enter_context(tc.psum_pool(name="psum", bufs=4))
+        psum_s = ctx.enter_context(tc.psum_pool(name="psum_s", bufs=3))
+        psum_z = ctx.enter_context(tc.psum_pool(name="psum_z", bufs=1))
+
+        def kept(name, shape, dtype):
+            return keep.tile(shape, dtype, name=name, align_bytes=64)
+
+        def bank():
+            return psum.tile([P, BANK], F32, name="bank")
+
+        def bank_s():
+            return psum_s.tile([P, BANK], F32, name="bank_s")
+
+        w_raw = kept("w_raw", [P, 2 * D], U8)
+        ws_raw = kept("ws_raw", [P, D], U8)
+        w_codes = kept("w_codes", [P, 2 * D], U8)
+        w_sc = kept("w_sc", [P, D], U8)
+        ident = kept("ident", [P, P], F32)
+        b_sb = kept("b_sb", [P, PACK], BF16)
+        wza_sb = kept("wza_sb", [P, PACK], BF16)
+        wzb_sb = kept("wzb_sb", [P, PACK], BF16)
+        warm_in = kept("warm_in", [P, 1], F32)
+        warm_out = kept("warm_out", [P, 1], F32)
+        y_scales = kept("y_scales", [P, GROUPS, B * M], U8)
+
+        nc.vector.memset(ws_raw[:].bitcast(I32), 0)
+        nc.vector.memset(warm_in[:], 0.0)
+        nc.scalar.activation(out=warm_out[:], in_=warm_in[:], func=ACT.Exp)
+        make_identity(nc, ident[:])
+        nc.gpsimd.dma_start(out=b_sb[:], in_=b.rearrange("(p t) -> p t", t=PACK))
+        nc.gpsimd.dma_start(out=wza_sb[:], in_=wza.rearrange("(p t) -> p t", t=PACK))
+        nc.gpsimd.dma_start(out=wzb_sb[:], in_=wzb.rearrange("(p t) -> p t", t=PACK))
+
+        raw = {}
+
+        def load_a(i, g, h):
+            raw[("a", i, g, h)] = kept("xa_%d%d%d" % (i, g, h), [P, 2, D], BF16)
+            rows = xa[i, g * BANK : (g + 1) * BANK, :].rearrange("(p t) d -> p t d", t=PACK)
+            nc.sync.dma_start(out=raw[("a", i, g, h)][:], in_=rows[:, 2 * h : 2 * h + 2, :])
+
+        def load_b(i, h):
+            raw[("b", i, h)] = kept("xb_%d%d" % (i, h), [P, 2, D], BF16)
+            rows = xb[i, 2 * P * h : 2 * P * (h + 1), :].rearrange("(j p) d -> p j d", p=P)
+            nc.sync.dma_start(out=raw[("b", i, h)][:], in_=rows)
+
+        load_a(0, 0, 0)
+        nc.sync.dma_start(out=w_raw[:].bitcast(I32), in_=w_words[0].bitcast(I32))
+        for quad in range(4):
+            nc.sync.dma_start(
+                out=ws_raw[32 * quad : 32 * quad + 4, :].bitcast(I32),
+                in_=w_scales[0, 4 * quad : 4 * quad + 4, :].bitcast(I32),
+            )
+        for i in range(B):
+            for g in range(GROUPS):
+                for h in range(2):
+                    if i + g + h > 0:
+                        load_a(i, g, h)
+            for h in range(3):
+                load_b(i, h)
+
+        nc.vector.tensor_copy(
+            out=w_codes[:].rearrange("p (t m e) -> p t m e", t=PACK, e=2),
+            in_=w_raw[:].rearrange("p (m t e) -> p t m e", t=PACK, e=2),
+        )
+        nc.vector.tensor_copy(
+            out=w_sc[:].rearrange("p (t m) -> p t m", t=PACK),
+            in_=ws_raw[:].rearrange("p (m t) -> p t m", t=PACK),
+        )
+
+        pending = []
+
+        def tick():
+            if pending:
+                pending[0]()
+                pending.remove(pending[0])
+
+        def quantize(codes, scales, grouped):
+            nc.vector.quantize_mx(out=codes.bitcast(FP8X4), scales=scales, in_=grouped)
+            tick()
+
+        def mx(out, lhs, lhs_sc, rhs, rhs_sc, lhs_dtype=FP8X4):
+            nc.tensor.matmul_mx(
+                out=out, lhsT=lhs.bitcast(lhs_dtype), lhsT_scale=lhs_sc,
+                rhs=rhs.bitcast(FP8X4), rhs_scale=rhs_sc, start=True, stop=True,
+            )
+
+        st = {}
+        for i in range(B):
+            for name in ("nbr", "sum", "x", "root", "r", "a0", "a1", "absz", "ez", "mz", "base", "term", "nterm"):
+                st[(name, i)] = kept("%s_%d" % (name, i), [P, STATS], F32)
+            st[("half", i)] = kept("half_%d" % i, [P, STATS, 2], F32)
+            st[("xb_c", i)] = kept("xb_c%d" % i, [P, M], U32)
+            st[("xb_s", i)] = kept("xb_s%d" % i, [P, M], U8)
+            st[("cb", i)] = kept("cb%d" % i, [P, M], F32)
+            for g in range(GROUPS):
+                for name in ("xa", "q"):
+                    st[(name + "_c", i, g)] = kept("%s_c%d%d" % (name, i, g), [P, BANK], U32)
+                    st[(name + "_s", i, g)] = kept("%s_s%d%d" % (name, i, g), [P, BANK], U8)
+                st[("y", i, g)] = kept("y%d%d" % (i, g), [P, PACK, M], F32)
+        inv_root = kept("inv_root", [P, STATS], F32)
+        nc.gpsimd.memset(inv_root[:], 1.0 / ROOT)
+        live = {}
+
+        def flush():
+            for k in range(len(pending)):
+                tick()
+
+        def nothing():
+            return None
+
+        def turn(key):
+            cols = slice(2 * P * key[-1], 2 * P * (key[-1] + 1))
+            dst = ("xa_c",) + key[1:3] if key[0] == "a" else ("xb_c", key[1])
+            dst_s = ("xa_s",) + key[1:3] if key[0] == "a" else ("xb_s", key[1])
+
+            def pe():
+                words = raw[key][:].rearrange("p a d -> p (a d)").bitcast(F32)
+                ps = bank_s()
+                live[key] = ps
+                for a in range(2):
+                    for u in range(2):
+                        k = 2 * a + u
+                        nc.tensor.transpose(
+                            ps[:, P * k : P * (k + 1)], words[:, 256 * a + u : 256 * (a + 1) : 2], ident[:]
+                        )
+
+            def out():
+                xt = kept("xt_" + "".join(str(s) for s in key), [P, 2 * P * PACK], BF16)
+                live[("xt",) + key] = xt
+                nc.scalar.copy(
+                    out=xt[:].bitcast(F32).rearrange("p (a r u) -> p a r u", a=2, u=2),
+                    in_=live[key][:].rearrange("p (a u r) -> p a r u", a=2, u=2),
+                )
+
+            def quant():
+                quantize(st[dst][:, cols], st[dst_s][:, cols], live[("xt",) + key][:])
+
+            return [pe, out, quant]
+
+        def logits(key, a):
+            i = key[1]
+            k = M_TILES + PACK * key[2] + 2 * key[3] + a if key[0] == "a" else 2 * key[2] + a
+            wz = wza_sb if key[0] == "a" else wzb_sb
+
+            def pe():
+                if ("z", i) not in live:
+                    live[("z", i)] = psum_z.tile([P, BANK], F32, name="z")
+                xt = live[("xt",) + key][:].rearrange("p (a r t) -> p a t r", a=2, t=PACK)
+                for t in range(PACK):
+                    nc.tensor.matmul(
+                        live[("z", i)][:, k : k + 1], lhsT=xt[:, a, t, :], rhs=wz[:, t : t + 1],
+                        start=(t == 0), stop=(t == PACK - 1),
+                    )
+
+            return pe
+
+        def project_tile(i, g, s):
+            cols = slice(P * s, P * (s + 1))
+            h, a = divmod(s, 2)
+
+            def pe():
+                ps = bank()
+                live[("p", i, g, s)] = ps
+                for t in range(PACK):
+                    mx(ps[:, P * t : P * (t + 1)], w_codes[:, 2 * P * t : 2 * P * (t + 1)],
+                       w_sc[:, P * t : P * (t + 1)], st[("xa_c", i, g)][:, cols], st[("xa_s", i, g)][:, cols], FP4X4)
+
+            def out():
+                if a == 0:
+                    live[("qg", i, g, h)] = rot.tile([P, 2 * P, PACK], BF16, name="qg", align_bytes=64)
+                nc.vector.tensor_tensor(
+                    out=live[("qg", i, g, h)][:, P * a : P * (a + 1), :],
+                    in0=live[("p", i, g, s)][:].rearrange("p (t n) -> p n t", t=PACK),
+                    in1=b_sb[:].unsqueeze(1).to_broadcast([P, P, PACK]),
+                    op=ALU.add,
+                )
+
+            return [pe, out, quant_q(i, g, h) if a == 1 else nothing]
+
+        def quant_q(i, g, h):
+            def quant():
+                cols = slice(2 * P * h, 2 * P * (h + 1))
+                quantize(st[("q_c", i, g)][:, cols], st[("q_s", i, g)][:, cols],
+                         live[("qg", i, g, h)][:].rearrange("p n t -> p (n t)"))
+
+            return quant
+
+        def project_slot(i, g, t):
+            def pe():
+                ps = bank_s()
+                live[("p", i, g, t)] = ps
+                mx(ps[:], w_codes[:, 2 * P * t : 2 * P * (t + 1)], w_sc[:, P * t : P * (t + 1)],
+                   st[("xa_c", i, g)][:], st[("xa_s", i, g)][:], FP4X4)
+
+            def out():
+                if t == 0:
+                    live[("qs", i, g)] = rot.tile([P, PACK, BANK], BF16, name="qs", align_bytes=64)
+                nc.scalar.activation(out=live[("qs", i, g)][:, t, :], in_=live[("p", i, g, t)][:],
+                                     func=ACT.Identity, bias=b_sb[:, t : t + 1])
+
+            return [pe, out, nothing]
+
+        def interleave_q(i, g, h):
+            def go():
+                cols = slice(2 * P * h, 2 * P * (h + 1))
+                live[("qg", i, g, h)] = rot.tile([P, 2 * P, PACK], BF16, name="qg", align_bytes=64)
+                nc.gpsimd.tensor_scalar(
+                    out=live[("qg", i, g, h)][:], in0=live[("qs", i, g)][:, :, cols].rearrange("p t n -> p n t"),
+                    scalar1=1.0, scalar2=0.0, op0=ALU.mult, op1=ALU.add,
+                )
+
+            return go
+
+        def matchability(i, lo, hi):
+            def first():
+                nc.scalar.activation(out=st[("absz", i)][:, lo:hi], in_=live[("z", i)][:, lo:hi], func=ACT.Abs)
+
+            def second():
+                nc.vector.tensor_scalar(
+                    out=st[("mz", i)][:, lo:hi], in0=live[("z", i)][:, lo:hi], scalar1=0.0, scalar2=HALF_CONST, op0=ALU.min, op1=ALU.add
+                )
+                nc.scalar.activation(out=st[("ez", i)][:, lo:hi], in_=st[("absz", i)][:, lo:hi], func=ACT.Exp, scale=-1.0)
+
+            return [only(first), only(second)]
+
+        def scores(src, dst, scale, first, acc):
+            nc.vector.tensor_scalar(out=dst, in0=src, scalar1=scale, scalar2=first, op0=ALU.mult, op1=ALU.min, accum_out=acc)
+            tick()
+
+        def row_pair(i, g, h):
+            y, half, nb = st[("y", i, g)], st[("half", i)], st[("nbr", i)]
+            t0, t1 = 2 * h, 2 * h + 1
+            k0, k1 = M_TILES + PACK * g + t0, M_TILES + PACK * g + t1
+
+            def pe():
+                ps = {}
+                live[("r", i, g, h)] = ps
+                for lo, hi in ((0, BANK), (BANK, M)):
+                    for t in (t0, t1):
+                        ps[(t, lo)] = bank()
+                        cols = slice(P * t, P * (t + 1))
+                        mx(ps[(t, lo)][:, 0 : hi - lo], st[("q_c", i, g)][:, cols], st[("q_s", i, g)][:, cols],
+                           st[("xb_c", i)][:, lo:hi], st[("xb_s", i)][:, lo:hi])
+
+            def peak():
+                ps = live[("r", i, g, h)]
+                scores(ps[(t0, 0)][:], y[:, t0, 0:BANK], -C, None, half[:, k0, 0:1])
+                scores(ps[(t1, 0)][:], y[:, t1, 0:BANK], -2.0 * C, None, half[:, k1, 0:1])
+                scores(ps[(t0, BANK)][:, 0 : M - BANK], y[:, t0, BANK:M], -C, half[:, k0, 0:1], nb[:, k0 : k0 + 1])
+                scores(ps[(t1, BANK)][:, 0 : M - BANK], y[:, t1, BANK:M], -2.0 * C, half[:, k1, 0:1], half[:, k1, 1:2])
+
+            def join():
+                nc.vector.tensor_scalar(out=nb[:, k1 : k1 + 1], in0=half[:, k1, 1:2], scalar1=0.5, scalar2=None, op0=ALU.mult)
+
+            def total(t, k, scale):
+                def go():
+                    junk = rot.tile([P, N], BF16, name="junk", bufs=3)
+                    nc.scalar.activation(
+                        out=junk[:, 0:M], in_=y[:, t, :], func=ACT.Exp, scale=scale, bias=nb[:, k : k + 1],
+                        accum_out=st[("sum", i)][:, k : k + 1],
+                    )
+
+                return go
+
+            return [pe, peak, join, total(t0, k0, -1.0), total(t1, k1, -0.5)]
+
+        def column_half(i, j, g):
+            half, nb = st[("half", i)], st[("nbr", i)]
+            cols = slice(P * j, P * (j + 1))
+
+            def pe():
+                ps = bank()
+                live[("c", i, j, g)] = ps
+                mx(ps[:], st[("xb_c", i)][:, cols], st[("xb_s", i)][:, cols], st[("q_c", i, g)][:], st[("q_s", i, g)][:])
+
+            def peak():
+                if g == 0:
+                    live[("st", i, j)] = kept("s_t%d%d" % (i, j), [P, N], F32)
+                scores(live[("c", i, j, g)][:], live[("st", i, j)][:, BANK * g : BANK * (g + 1)], -C,
+                       half[:, j, 0:1] if g else None, nb[:, j : j + 1] if g else half[:, j, 0:1])
+
+            def total():
+                junk = rot.tile([P, N], BF16, name="junk", bufs=3)
+                nc.scalar.activation(
+                    out=junk[:], in_=live[("st", i, j)][:], func=ACT.Exp, scale=-1.0, bias=nb[:, j : j + 1],
+                    accum_out=st[("sum", i)][:, j : j + 1],
+                )
+
+            return [pe, peak, total]
+
+        def terms(i, lo, hi, wait):
+            def s(name):
+                return st[(name, i)][:, lo:hi]
+
+            def begin():
+                nc.vector.scalar_tensor_tensor(out=s("x"), in0=s("ez"), scalar=1.0, in1=s("sum"), op0=ALU.add, op1=ALU.mult)
+                nc.gpsimd.tensor_tensor(out=s("root"), in0=s("x"), in1=inv_root[:, lo:hi], op=ALU.pow)
+                nc.vector.tensor_tensor(out=s("base"), in0=s("nbr"), in1=s("mz"), op=ALU.add)
+
+            def start():
+                nc.vector.tensor_scalar(out=s("r"), in0=s("root"), scalar1=-1.0, scalar2=None, op0=ALU.add)
+                nc.vector.tensor_scalar(out=s("a0"), in0=s("root"), scalar1=-1.0, scalar2=ROOT / 5.0, op0=ALU.add, op1=ALU.mult)
+
+            def horner(src, dst, coef):
+                return lambda: nc.vector.scalar_tensor_tensor(out=s(dst), in0=s(src), scalar=coef, in1=s("r"), op0=ALU.add, op1=ALU.mult)
+
+            def end():
+                nc.vector.tensor_tensor(out=s("term"), in0=s("base"), in1=s("a0"), op=ALU.subtract)
+
+            def negate():
+                nc.vector.tensor_scalar(out=st[("nterm", i)][:, 0:M_TILES], in0=st[("term", i)][:, 0:M_TILES],
+                                        scalar1=-0.5, scalar2=None, op0=ALU.mult)
+
+            steps = [begin] + [nothing] * wait + [start, horner("a0", "a1", -ROOT / 4.0), horner("a1", "a0", ROOT / 3.0),
+                                                  horner("a0", "a1", -ROOT / 2.0), horner("a1", "a0", ROOT), end]
+            if lo == 0:
+                steps.append(negate)
+            return lambda: pending.extend(steps)
+
+        def spread(i):
+            def pe():
+                ps = [bank_s(), bank_s()]
+                live[("cb", i)] = ps
+                for j in range(M_TILES):
+                    nc.tensor.transpose(
+                        ps[j // 4][:, P * (j % 4) : P * (j % 4 + 1)],
+                        st[("term", i)][:, j : j + 1].to_broadcast([P, P]), ident[:],
+                    )
+
+            def out():
+                ps = live[("cb", i)]
+                nc.scalar.copy(out=st[("cb", i)][:, 0:BANK], in_=ps[0][:])
+                nc.scalar.copy(out=st[("cb", i)][:, BANK:M], in_=ps[1][:, 0 : M - BANK])
+
+            return [pe, out]
+
+        def result_tile(i, g, t):
+            def add():
+                y = st[("y", i, g)]
+                rows = out_0[i, g * BANK : (g + 1) * BANK, :].rearrange("(p t) m -> p t m", t=PACK)
+                k = M_TILES + PACK * g + t
+                nc.vector.scalar_tensor_tensor(
+                    out=y[:, t, :], in0=st[("cb", i)][:], scalar=st[("term", i)][:, k : k + 1], in1=y[:, t, :],
+                    op0=ALU.add, op1=ALU.subtract,
+                )
+                tick()
+                nc.sync.dma_start(out=rows[:, t, :], in_=y[:, t, :])
+
+            return [nothing, add]
+
+        def result_turned(i, g, t):
+            k = M_TILES + PACK * g + t
+            cols = slice(BANK * g + P * t, BANK * g + P * (t + 1))
+
+            def pe():
+                ps = [bank_s(), bank_s()]
+                live[("e", i, g, t)] = ps
+                for j in range(M_TILES):
+                    dst = ps[j // 4][:, P * (j % 4) : P * (j % 4 + 1)]
+                    nc.tensor.matmul(dst, lhsT=live[("st", i, j)][:, cols], rhs=ident[:], is_transpose=True, start=True, stop=False)
+                    nc.tensor.matmul(dst, lhsT=st[("nterm", i)][:, j : j + 1].to_broadcast([P, P]), rhs=ident[:],
+                                     is_transpose=True, start=False, stop=True)
+
+            def add():
+                y, ps = st[("y", i, g)], live[("e", i, g, t)]
+                rows = out_0[i, g * BANK : (g + 1) * BANK, :].rearrange("(p t) m -> p t m", t=PACK)
+                for src, part in ((ps[0][:], slice(0, BANK)), (ps[1][:, 0 : M - BANK], slice(BANK, M))):
+                    nc.scalar.activation(out=y[:, t, part], in_=src, func=ACT.Identity, scale=-2.0, bias=st[("term", i)][:, k : k + 1])
+                nc.sync.dma_start(out=rows[:, t, :], in_=y[:, t, :])
+
+            return [pe, add]
+
+        def plane_chunk(i, g, k, eng):
+            cols = slice(256 * k, 256 * (k + 1))
+
+            def pack():
+                yb = rot.tile([P, 256, PACK], BF16, name="yb", bufs=6, align_bytes=64)
+                live[("yb", i, g, k)] = yb
+                dst = yb[:].rearrange("p (c e) t -> p c t e", e=4)
+                src = st[("y", i, g)][:, :, cols].rearrange("p t (c e) -> p c t e", e=4)
+                if eng == "S":
+                    nc.scalar.copy(out=dst, in_=src)
+                elif eng == "V":
+                    nc.vector.tensor_copy(out=dst, in_=src)
+                    tick()
+                else:
+                    nc.gpsimd.tensor_scalar(out=yb[:], in0=st[("y", i, g)][:, :, cols].rearrange("p t m -> p m t"),
+                                            scalar1=1.0, scalar2=0.0, op0=ALU.mult, op1=ALU.add)
+
+            def quant():
+                if ("yc", i, g) not in live:
+                    live[("left", i, g)] = [0, 1, 2]
+                    live[("yc", i, g)] = rot.tile([P, M], U32, name="y_codes", align_bytes=64)
+                codes = live[("yc", i, g)]
+                quantize(codes[:, cols], y_scales[:, g, M * i + 256 * k : M * i + 256 * (k + 1)],
+                         live[("yb", i, g, k)][:].rearrange("p m t -> p (m t)"))
+                live[("left", i, g)].remove(k)
+                if not live[("left", i, g)]:
+                    nc.sync.dma_start(
+                        out=out_1[g, :, M * i : M * (i + 1), :].rearrange("p m t -> p (m t)").bitcast(I32),
+                        in_=codes[:].bitcast(I32),
+                    )
+
+            return [nothing, pack, quant]
+
+        def run(slots):
+            for k in range(-1, len(slots)):
+                if k >= 0:
+                    for pe, main in slots[k]:
+                        main()
+                if k + 1 < len(slots):
+                    for pe, main in slots[k + 1]:
+                        pe()
+
+        ROWNB = nc.vector
+
+        def keys(i):
+            return [("a", i, 0, 0), ("a", i, 0, 1), ("a", i, 1, 0), ("a", i, 1, 1), ("b", i, 0), ("b", i, 1), ("b", i, 2)]
+
+        k0, k1 = keys(0), keys(1)
+
+        def lead(unit):
+            return (unit[0], unit[1])
+
+        def late(unit, n):
+            return (nothing, unit[n])
+
+        def only(thunk):
+            return (nothing, thunk)
+
+        def T(key):
+            return lead(turn(key))
+
+        def TQ(key):
+            return late(turn(key), 2)
+
+        def PV(i, g, s):
+            return lead(project_tile(i, g, s))
+
+        def QQ(i, g, h):
+            return only(quant_q(i, g, h))
+
+        def A(i, g, h):
+            return lead(row_pair(i, g, h))
+
+        def J(i, g, h):
+            return late(row_pair(i, g, h), 2)
+
+        def BB(i, g, t):
+            return late(row_pair(i, g, t // 2), 3 + t % 2)
+
+        def CC(i, j, g):
+            return lead(column_half(i, j, g))
+
+        def DD(i, j):
+            return late(column_half(i, j, 1), 2)
+
+        def PS(i, g, t):
+            return lead(project_slot(i, g, t))
+
+        def IL(i, g, h):
+            return only(interleave_q(i, g, h))
+
+        def columns(i):
+            return [[CC(i, 0, 0)]] + [[CC(i, j + 1, 0), CC(i, j, 1)] for j in range(5)] + [[CC(i, 5, 1)]]
+
+        def EV(i, g, t):
+            return lead(result_tile(i, g, t))
+
+        def ES(i, g, t):
+            return lead(result_turned(i, g, t))
+
+        def F(i, g, k, eng):
+            return lead(plane_chunk(i, g, k, eng))
+
+        def FQ(i, g, k):
+            return late(plane_chunk(i, g, k, "S"), 2)
+
+        def put(slots, start, items, step=1):
+            for n, item in enumerate(items):
+                while len(slots) <= start + n * step:
+                    slots.append([])
+                slots[start + n * step].extend(item if isinstance(item, list) else [item])
+
+        def Z(key, e):
+            return (logits(key, e), nothing)
+
+        def ZZ(key):
+            return [Z(key, 0), Z(key, 1)]
+
+        slots = [
+            [T(k0[0])], [T(k0[1])], [T(k0[2]), TQ(k0[0])], [PV(0, 0, 0), TQ(k0[1]), PV(0, 0, 1), T(k0[3])],
+            [PV(0, 0, 2), QQ(0, 0, 0), TQ(k0[2]), PV(0, 0, 3), T(k0[4])],
+            [PV(0, 1, 0), TQ(k0[3]), QQ(0, 0, 1), PV(0, 1, 1), T(k0[5])],
+            [PV(0, 1, 2), TQ(k0[4]), QQ(0, 1, 0), PV(0, 1, 3), T(k0[6])],
+            [TQ(k0[5]), QQ(0, 1, 1), T(k1[0])],
+        ]
+        c0 = len(slots)
+        put(slots, c0, columns(0))
+        put(slots, c0, [[TQ(k0[6]), T(k1[1])], [TQ(k1[0]), T(k1[2])], [TQ(k1[1]), T(k1[3]), DD(0, 0)], [TQ(k1[2]), DD(0, 1)], [TQ(k1[3]), DD(0, 2)],
+                        [DD(0, 3), PS(1, 0, 0)], [DD(0, 4), PS(1, 0, 1)]])
+        put(slots, c0 + 2, [Z(key, e) for key in k0[4:] for e in range(2)][:5])
+        slots += [
+            [A(0, 0, 0), DD(0, 5), PS(1, 0, 2), PS(1, 0, 3), IL(1, 0, 0), IL(1, 0, 1), Z(k0[6], 1)] + ZZ(k0[0]),
+            [A(0, 0, 1), J(0, 0, 0), BB(0, 0, 0), BB(0, 0, 1), PS(1, 1, 0)] + ZZ(k0[1]),
+            [A(0, 1, 0), J(0, 0, 1)] + matchability(0, 0, 10) + [BB(0, 0, 2), BB(0, 0, 3), QQ(1, 0, 0), PS(1, 1, 1), PS(1, 1, 2), PS(1, 1, 3), only(terms(0, 0, 10, 3))] + ZZ(k0[2]),
+            [A(0, 1, 1), J(0, 1, 0), QQ(1, 0, 1), IL(1, 1, 0), IL(1, 1, 1), BB(0, 1, 0), BB(0, 1, 1), T(k1[4])] + ZZ(k0[3]),
+            [J(0, 1, 1)] + matchability(0, 10, 14) + [BB(0, 1, 2), BB(0, 1, 3), T(k1[5]), T(k1[6]), TQ(k1[4]), QQ(1, 1, 0), TQ(k1[5]), QQ(1, 1, 1), only(flush)],
+        ]
+        c1 = len(slots)
+        put(slots, c1, [[only(terms(0, 10, STATS, 2))], TQ(k1[6])])
+        put(slots, c1, columns(1))
+        put(slots, c1, [lead(spread(0)), ES(0, 0, 0), [ES(0, 0, 2), EV(0, 0, 1)], [DD(1, 0), EV(0, 0, 3)], [DD(1, 1), only(flush)], [DD(1, 2), ES(0, 1, 0)], [DD(1, 3), EV(0, 1, 1)]])
+        put(slots, c1 + 2, [Z(key, e) for key in k1[4:] for e in range(2)][:5])
+        slots += [
+            [A(1, 0, 0), DD(1, 4), DD(1, 5), Z(k1[6], 1)] + ZZ(k1[0]),
+            [A(1, 0, 1), J(1, 0, 0), BB(1, 0, 0), BB(1, 0, 1), ES(0, 1, 2), EV(0, 1, 3)] + ZZ(k1[1]),
+            [A(1, 1, 0), J(1, 0, 1)] + matchability(1, 0, 10) + [BB(1, 0, 2), BB(1, 0, 3), F(0, 0, 0, "S"), only(terms(1, 0, 10, 3))] + ZZ(k1[2]),
+            [A(1, 1, 1), J(1, 1, 0), BB(1, 1, 0), BB(1, 1, 1), FQ(0, 0, 0)] + ZZ(k1[3]),
+            [J(1, 1, 1)] + matchability(1, 10, 14) + [BB(1, 1, 2), BB(1, 1, 3), F(0, 0, 1, "S"), F(0, 0, 2, "S"), FQ(0, 0, 1), F(0, 1, 0, "S"), FQ(0, 0, 2), only(flush)],
+            [only(terms(1, 10, STATS, 2)), lead(spread(1)), F(0, 1, 1, "V"), FQ(0, 1, 0), F(0, 1, 2, "V"), FQ(0, 1, 1)],
+            [ES(1, 0, 0), EV(1, 0, 1), FQ(0, 1, 2)], [ES(1, 0, 2), EV(1, 0, 3), only(flush)],
+            [ES(1, 1, 0), EV(1, 1, 1), F(1, 0, 1, "V")], [ES(1, 1, 2), EV(1, 1, 3), F(1, 0, 2, "V"), F(1, 0, 0, "S"), FQ(1, 0, 1)],
+            [F(1, 1, 0, "S"), F(1, 1, 1, "V"), FQ(1, 0, 2), F(1, 1, 2, "V"), FQ(1, 0, 0)], [FQ(1, 1, 1), FQ(1, 1, 2), FQ(1, 1, 0)],
+        ]
+        run(slots)
+        for quad in range(4):
+            nc.sync.dma_start(
+                out=out_2[:, 4 * quad : 4 * quad + 4, :].rearrange("g r m -> r g m").bitcast(I32),
+                in_=y_scales[32 * quad : 32 * quad + 4, :, :].bitcast(I32),
+            )

@@ -26,7 +26,8 @@ M_TILES = M // P
 STATS = M_TILES + GROUPS * PACK
 C = 1.0 / math.sqrt(D)
 HALF_CONST = 0.5 * (math.log(N) + math.log(M))
-ROOT = 512.0
+LN2 = math.log(2.0)
+GUESS_SHIFT = 0.043
 
 
 def tile_lightgluematchabilityassignment_x2_kernel(
@@ -64,10 +65,15 @@ def tile_lightgluematchabilityassignment_x2_kernel(
         nc.vector.memset(ws_raw[:].bitcast(I32), 0)
         nc.vector.memset(warm_in[:], 0.0)
         nc.scalar.activation(out=warm_out[:], in_=warm_in[:], func=ACT.Exp)
-        make_identity(nc, ident[:])
-        nc.gpsimd.dma_start(out=b_sb[:], in_=b.rearrange("(p t) -> p t", t=PACK))
-        nc.gpsimd.dma_start(out=wza_sb[:], in_=wza.rearrange("(p t) -> p t", t=PACK))
-        nc.gpsimd.dma_start(out=wzb_sb[:], in_=wzb.rearrange("(p t) -> p t", t=PACK))
+        gather = kept("gather", [P, 224], F32)
+        with tc.manual_schedule(engines={mybir.EngineType.Pool}):
+            make_identity(nc, ident[:])
+            nc.gpsimd.dma_start(out=b_sb[:], in_=b.rearrange("(p t) -> p t", t=PACK))
+            nc.gpsimd.memset(gather[:], 1.0)
+            nc.gpsimd.affine_select(out=gather[:], in_=gather[:], compare_op=ALU.is_ge, fill=0.0, base=4 * 96, pattern=[[-4, 224]], channel_multiplier=1)
+            nc.gpsimd.affine_select(out=gather[:], in_=gather[:], compare_op=ALU.is_ge, fill=0.0, base=3 - 4 * 96, pattern=[[4, 224]], channel_multiplier=-1)
+            nc.gpsimd.dma_start(out=wza_sb[:], in_=wza.rearrange("(p t) -> p t", t=PACK))
+            nc.gpsimd.dma_start(out=wzb_sb[:], in_=wzb.rearrange("(p t) -> p t", t=PACK))
 
         raw = {}
 
@@ -81,20 +87,22 @@ def tile_lightgluematchabilityassignment_x2_kernel(
             rows = xb[i, 2 * P * h : 2 * P * (h + 1), :].rearrange("(j p) d -> p j d", p=P)
             nc.sync.dma_start(out=raw[("b", i, h)][:], in_=rows)
 
-        load_a(0, 0, 0)
-        nc.sync.dma_start(out=w_raw[:].bitcast(I32), in_=w_words[0].bitcast(I32))
-        for quad in range(4):
-            nc.sync.dma_start(
-                out=ws_raw[32 * quad : 32 * quad + 4, :].bitcast(I32),
-                in_=w_scales[0, 4 * quad : 4 * quad + 4, :].bitcast(I32),
-            )
-        for i in range(B):
-            for g in range(GROUPS):
-                for h in range(2):
-                    if i + g + h > 0:
-                        load_a(i, g, h)
+        with tc.manual_schedule(engines={mybir.EngineType.SP}):
+            load_a(0, 0, 0)
+            nc.sync.dma_start(out=w_raw[:].bitcast(I32), in_=w_words[0].bitcast(I32))
+            load_a(0, 0, 1)
+            for quad in range(4):
+                nc.sync.dma_start(
+                    out=ws_raw[32 * quad : 32 * quad + 4, :].bitcast(I32),
+                    in_=w_scales[0, 4 * quad : 4 * quad + 4, :].bitcast(I32),
+                )
             for h in range(3):
-                load_b(i, h)
+                load_b(0, h)
+            for i, g in ((0, 1), (1, 0), (1, 1)):
+                for h in range(2):
+                    load_a(i, g, h)
+            for h in range(3):
+                load_b(1, h)
 
         nc.vector.tensor_copy(
             out=w_codes[:].rearrange("p (t m e) -> p t m e", t=PACK, e=2),
@@ -124,20 +132,20 @@ def tile_lightgluematchabilityassignment_x2_kernel(
 
         st = {}
         for i in range(B):
-            for name in ("nbr", "sum", "x", "root", "r", "a0", "a1", "absz", "ez", "mz", "base", "term", "nterm"):
+            for name in ("nbr", "sum", "x", "ny0", "ny1", "ex", "u", "r", "a0", "a1", "absz", "ez", "mz", "base", "term", "nterm"):
                 st[(name, i)] = kept("%s_%d" % (name, i), [P, STATS], F32)
             st[("half", i)] = kept("half_%d" % i, [P, STATS, 2], F32)
             st[("xb_c", i)] = kept("xb_c%d" % i, [P, M], U32)
             st[("xb_s", i)] = kept("xb_s%d" % i, [P, M], U8)
-            st[("cb", i)] = kept("cb%d" % i, [P, M], F32)
             for g in range(GROUPS):
                 for name in ("xa", "q"):
                     st[(name + "_c", i, g)] = kept("%s_c%d%d" % (name, i, g), [P, BANK], U32)
                     st[(name + "_s", i, g)] = kept("%s_s%d%d" % (name, i, g), [P, BANK], U8)
                 st[("y", i, g)] = kept("y%d%d" % (i, g), [P, PACK, M], F32)
-        inv_root = kept("inv_root", [P, STATS], F32)
-        nc.gpsimd.memset(inv_root[:], 1.0 / ROOT)
+        own_slot = kept("own_slot", [P, PACK], F32)
+        nc.vector.tensor_reduce(out=own_slot[:], in_=ident[:].rearrange("p (a t) -> p t a", t=PACK), axis=AXIS.X, op=ALU.add)
         live = {}
+        z_bank = psum_z.tile([P, BANK], F32, name="z")
 
         def flush():
             for k in range(len(pending)):
@@ -181,14 +189,11 @@ def tile_lightgluematchabilityassignment_x2_kernel(
             wz = wza_sb if key[0] == "a" else wzb_sb
 
             def pe():
-                if ("z", i) not in live:
-                    live[("z", i)] = psum_z.tile([P, BANK], F32, name="z")
-                xt = live[("xt",) + key][:].rearrange("p (a r t) -> p a t r", a=2, t=PACK)
-                for t in range(PACK):
-                    nc.tensor.matmul(
-                        live[("z", i)][:, k : k + 1], lhsT=xt[:, a, t, :], rhs=wz[:, t : t + 1],
-                        start=(t == 0), stop=(t == PACK - 1),
-                    )
+                for q in range(4):
+                    col = PACK * (STATS * (4 * i + q) + k)
+                    lo = BANK * a + P * q
+                    nc.tensor.matmul(z_bank[:, col : col + PACK], lhsT=live[("xt",) + key][:, lo : lo + P], rhs=wz[:],
+                                     start=True, stop=True)
 
             return pe
 
@@ -199,13 +204,14 @@ def tile_lightgluematchabilityassignment_x2_kernel(
             def pe():
                 ps = bank()
                 live[("p", i, g, s)] = ps
-                for t in range(PACK):
-                    mx(ps[:, P * t : P * (t + 1)], w_codes[:, 2 * P * t : 2 * P * (t + 1)],
-                       w_sc[:, P * t : P * (t + 1)], st[("xa_c", i, g)][:, cols], st[("xa_s", i, g)][:, cols], FP4X4)
+                with tc.high_priority():
+                    for t in range(PACK):
+                        mx(ps[:, P * t : P * (t + 1)], w_codes[:, 2 * P * t : 2 * P * (t + 1)],
+                           w_sc[:, P * t : P * (t + 1)], st[("xa_c", i, g)][:, cols], st[("xa_s", i, g)][:, cols], FP4X4)
 
             def out():
                 if a == 0:
-                    live[("qg", i, g, h)] = rot.tile([P, 2 * P, PACK], BF16, name="qg", align_bytes=64)
+                    live[("qg", i, g, h)] = rot.tile([P, 2 * P, PACK], BF16, name="qg", bufs=4, align_bytes=64)
                 nc.vector.tensor_tensor(
                     out=live[("qg", i, g, h)][:, P * a : P * (a + 1), :],
                     in0=live[("p", i, g, s)][:].rearrange("p (t n) -> p n t", t=PACK),
@@ -232,63 +238,85 @@ def tile_lightgluematchabilityassignment_x2_kernel(
 
             def out():
                 if t == 0:
-                    live[("qs", i, g)] = rot.tile([P, PACK, BANK], BF16, name="qs", align_bytes=64)
+                    live[("qs", i, g)] = rot.tile([P, PACK, BANK], BF16, name="qs", bufs=2, align_bytes=64)
                 nc.scalar.activation(out=live[("qs", i, g)][:, t, :], in_=live[("p", i, g, t)][:],
                                      func=ACT.Identity, bias=b_sb[:, t : t + 1])
 
             return [pe, out, nothing]
 
-        def interleave_q(i, g, h):
+        def interleave_q(i, g, h, eng):
             def go():
                 cols = slice(2 * P * h, 2 * P * (h + 1))
-                live[("qg", i, g, h)] = rot.tile([P, 2 * P, PACK], BF16, name="qg", align_bytes=64)
-                nc.gpsimd.tensor_scalar(
-                    out=live[("qg", i, g, h)][:], in0=live[("qs", i, g)][:, :, cols].rearrange("p t n -> p n t"),
-                    scalar1=1.0, scalar2=0.0, op0=ALU.mult, op1=ALU.add,
-                )
+                live[("qg", i, g, h)] = rot.tile([P, 2 * P, PACK], BF16, name="qg", bufs=4, align_bytes=64)
+                if eng == "G":
+                    nc.gpsimd.tensor_scalar(
+                        out=live[("qg", i, g, h)][:], in0=live[("qs", i, g)][:, :, cols].rearrange("p t n -> p n t"),
+                        scalar1=1.0, scalar2=0.0, op0=ALU.mult, op1=ALU.add,
+                    )
+                else:
+                    nc.vector.tensor_copy(
+                        out=live[("qg", i, g, h)][:].rearrange("p (c e) t -> p c t e", e=4),
+                        in_=live[("qs", i, g)][:, :, cols].rearrange("p t (c e) -> p c t e", e=4),
+                    )
+                    tick()
 
             return go
 
-        def matchability(i, lo, hi):
-            def first():
-                nc.scalar.activation(out=st[("absz", i)][:, lo:hi], in_=live[("z", i)][:, lo:hi], func=ACT.Abs)
+        def matchability(i):
+            n = 4 * STATS
+            zm = kept("zm%d" % i, [P, n, PACK], F32)
+            zz = kept("zz%d" % i, [P, n], F32)
+            z = z_bank[:, B * PACK * n + STATS * i : B * PACK * n + STATS * (i + 1)]
+            absz, ez, mz = st[("absz", i)], st[("ez", i)], st[("mz", i)]
 
-            def second():
-                nc.vector.tensor_scalar(
-                    out=st[("mz", i)][:, lo:hi], in0=live[("z", i)][:, lo:hi], scalar1=0.0, scalar2=HALF_CONST, op0=ALU.min, op1=ALU.add
+            def pick():
+                nc.vector.tensor_tensor(
+                    out=zm[:], in0=z_bank[:, PACK * n * i : PACK * n * (i + 1)].rearrange("p (c t) -> p c t", t=PACK),
+                    in1=own_slot[:].unsqueeze(1).to_broadcast([P, n, PACK]), op=ALU.mult,
                 )
-                nc.scalar.activation(out=st[("ez", i)][:, lo:hi], in_=st[("absz", i)][:, lo:hi], func=ACT.Exp, scale=-1.0)
 
-            return [only(first), only(second)]
+            def fold():
+                nc.vector.tensor_reduce(out=zz[:], in_=zm[:], axis=AXIS.X, op=ALU.add)
+                for q in range(4):
+                    nc.tensor.matmul(z, lhsT=gather[:, 96 - 32 * q : 224 - 32 * q], rhs=zz[:, STATS * q : STATS * (q + 1)],
+                                     start=(q == 0), stop=(q == 3))
+
+            def size():
+                nc.scalar.activation(out=absz[:], in_=z, func=ACT.Abs)
+
+            def low():
+                nc.vector.tensor_scalar(out=mz[:], in0=z, scalar1=0.0, scalar2=HALF_CONST, op0=ALU.min, op1=ALU.add)
+
+            def decay():
+                nc.scalar.activation(out=ez[:], in_=absz[:], func=ACT.Exp, scale=-1.0)
+
+            return [pick, fold, size, low, decay]
 
         def scores(src, dst, scale, first, acc):
             nc.vector.tensor_scalar(out=dst, in0=src, scalar1=scale, scalar2=first, op0=ALU.mult, op1=ALU.min, accum_out=acc)
             tick()
 
         def row_pair(i, g, h):
+            turned = (i, g, h) in TURNED
+            s0 = -C if turned else -2.0 * C
             y, half, nb = st[("y", i, g)], st[("half", i)], st[("nbr", i)]
             t0, t1 = 2 * h, 2 * h + 1
             k0, k1 = M_TILES + PACK * g + t0, M_TILES + PACK * g + t1
 
-            def pe():
-                ps = {}
-                live[("r", i, g, h)] = ps
-                for lo, hi in ((0, BANK), (BANK, M)):
-                    for t in (t0, t1):
-                        ps[(t, lo)] = bank()
-                        cols = slice(P * t, P * (t + 1))
-                        mx(ps[(t, lo)][:, 0 : hi - lo], st[("q_c", i, g)][:, cols], st[("q_s", i, g)][:, cols],
+            def part(t, k, lo, hi, scale, first, acc):
+                def go():
+                    ps = bank()
+                    cols = slice(P * t, P * (t + 1))
+                    with tc.high_priority():
+                        mx(ps[:, 0 : hi - lo], st[("q_c", i, g)][:, cols], st[("q_s", i, g)][:, cols],
                            st[("xb_c", i)][:, lo:hi], st[("xb_s", i)][:, lo:hi])
+                    scores(ps[:, 0 : hi - lo], y[:, t, lo:hi], scale, first, acc)
 
-            def peak():
-                ps = live[("r", i, g, h)]
-                scores(ps[(t0, 0)][:], y[:, t0, 0:BANK], -C, None, half[:, k0, 0:1])
-                scores(ps[(t1, 0)][:], y[:, t1, 0:BANK], -2.0 * C, None, half[:, k1, 0:1])
-                scores(ps[(t0, BANK)][:, 0 : M - BANK], y[:, t0, BANK:M], -C, half[:, k0, 0:1], nb[:, k0 : k0 + 1])
-                scores(ps[(t1, BANK)][:, 0 : M - BANK], y[:, t1, BANK:M], -2.0 * C, half[:, k1, 0:1], half[:, k1, 1:2])
+                return go
 
             def join():
-                nc.vector.tensor_scalar(out=nb[:, k1 : k1 + 1], in0=half[:, k1, 1:2], scalar1=0.5, scalar2=None, op0=ALU.mult)
+                lo = k1 if turned else k0
+                nc.scalar.activation(out=nb[:, lo : k1 + 1], in_=half[:, lo : k1 + 1, 1], func=ACT.Copy, scale=0.5)
 
             def total(t, k, scale):
                 def go():
@@ -300,7 +328,10 @@ def tile_lightgluematchabilityassignment_x2_kernel(
 
                 return go
 
-            return [pe, peak, join, total(t0, k0, -1.0), total(t1, k1, -0.5)]
+            return [part(t0, k0, 0, BANK, s0, None, half[:, k0, 0:1]), part(t1, k1, 0, BANK, -2.0 * C, None, half[:, k1, 0:1]),
+                    part(t0, k0, BANK, M, s0, half[:, k0, 0:1], nb[:, k0 : k0 + 1] if turned else half[:, k0, 1:2]),
+                    part(t1, k1, BANK, M, -2.0 * C, half[:, k1, 0:1], half[:, k1, 1:2]),
+                    both(join, total(t0, k0, -1.0 if turned else -0.5)), total(t1, k1, -0.5)]
 
         def column_half(i, j, g):
             half, nb = st[("half", i)], st[("nbr", i)]
@@ -309,11 +340,12 @@ def tile_lightgluematchabilityassignment_x2_kernel(
             def pe():
                 ps = bank()
                 live[("c", i, j, g)] = ps
-                mx(ps[:], st[("xb_c", i)][:, cols], st[("xb_s", i)][:, cols], st[("q_c", i, g)][:], st[("q_s", i, g)][:])
+                with tc.high_priority():
+                    mx(ps[:], st[("xb_c", i)][:, cols], st[("xb_s", i)][:, cols], st[("q_c", i, g)][:], st[("q_s", i, g)][:])
 
             def peak():
                 if g == 0:
-                    live[("st", i, j)] = kept("s_t%d%d" % (i, j), [P, N], F32)
+                    live[("st", i, j)] = rot.tile([P, N], F32, name="s_t", bufs=12 if TURNED else 5)
                 scores(live[("c", i, j, g)][:], live[("st", i, j)][:, BANK * g : BANK * (g + 1)], -C,
                        half[:, j, 0:1] if g else None, nb[:, j : j + 1] if g else half[:, j, 0:1])
 
@@ -326,38 +358,63 @@ def tile_lightgluematchabilityassignment_x2_kernel(
 
             return [pe, peak, total]
 
-        def terms(i, lo, hi, wait):
+        def terms(i, lo, hi):
             def s(name):
                 return st[(name, i)][:, lo:hi]
 
-            def begin():
+            def two(dst, a, z, op):
+                return lambda: nc.vector.tensor_tensor(out=s(dst), in0=s(a), in1=s(z), op=op)
+
+            def affine(dst, src, first, second, op0, op1):
+                return lambda: nc.vector.tensor_scalar(out=s(dst), in0=s(src), scalar1=first, scalar2=second, op0=op0, op1=op1)
+
+            def horner(dst, src, coef, other):
+                return lambda: nc.vector.scalar_tensor_tensor(out=s(dst), in0=s(src), scalar=coef, in1=s(other), op0=ALU.add, op1=ALU.mult)
+
+            def exp_of(src):
+                return lambda: nc.scalar.activation(out=s("ex"), in_=s(src), func=ACT.Exp)
+
+            def guess():
+                nc.vector.tensor_scalar(
+                    out=s("ny0"), in0=s("x").bitcast(I32), scalar1=-LN2 / 2.0**23, scalar2=(127.0 - GUESS_SHIFT) * LN2,
+                    op0=ALU.mult, op1=ALU.add,
+                )
+
+            steps = [
+                horner("x", "ez", 1.0, "sum"),
+                guess,
+                two("base", "nbr", "mz", ALU.add),
+                two("u", "x", "ex", ALU.mult),
+                affine("a0", "u", -0.5, 1.5, ALU.mult, ALU.add),
+                horner("a1", "u", -1.0, "a0"),
+                two("ny1", "ny0", "a1", ALU.subtract),
+                two("base", "base", "ny1", ALU.add),
+                two("u", "x", "ex", ALU.mult),
+                both(affine("r", "u", 1.0, -1.0, ALU.mult, ALU.add), affine("a0", "u", -1.0, -0.25, ALU.add, ALU.mult)),
+                horner("a1", "a0", 1.0 / 3.0, "r"),
+                horner("a0", "a1", -0.5, "r"),
+                horner("a1", "a0", 1.0, "r"),
+                two("term", "base", "a1", ALU.subtract),
+            ]
+            if lo == 0:
+                steps.append(lambda: nc.vector.tensor_scalar(out=st[("nterm", i)][:, 0:M_TILES], in0=st[("term", i)][:, 0:M_TILES],
+                                                             scalar1=-0.5, scalar2=None, op0=ALU.mult))
+            return steps, [exp_of("ny0"), exp_of("ny1")]
+
+        def terms_ln(i, lo, hi):
+            def s(name):
+                return st[(name, i)][:, lo:hi]
+
+            def first():
                 nc.vector.scalar_tensor_tensor(out=s("x"), in0=s("ez"), scalar=1.0, in1=s("sum"), op0=ALU.add, op1=ALU.mult)
-                nc.gpsimd.tensor_tensor(out=s("root"), in0=s("x"), in1=inv_root[:, lo:hi], op=ALU.pow)
                 nc.vector.tensor_tensor(out=s("base"), in0=s("nbr"), in1=s("mz"), op=ALU.add)
 
-            def start():
-                nc.vector.tensor_scalar(out=s("r"), in0=s("root"), scalar1=-1.0, scalar2=None, op0=ALU.add)
-                nc.vector.tensor_scalar(out=s("a0"), in0=s("root"), scalar1=-1.0, scalar2=ROOT / 5.0, op0=ALU.add, op1=ALU.mult)
-
-            def horner(src, dst, coef):
-                return lambda: nc.vector.scalar_tensor_tensor(out=s(dst), in0=s(src), scalar=coef, in1=s("r"), op0=ALU.add, op1=ALU.mult)
-
-            def end():
-                nc.vector.tensor_tensor(out=s("term"), in0=s("base"), in1=s("a0"), op=ALU.subtract)
-
-            def negate():
-                nc.vector.tensor_scalar(out=st[("nterm", i)][:, 0:M_TILES], in0=st[("term", i)][:, 0:M_TILES],
-                                        scalar1=-0.5, scalar2=None, op0=ALU.mult)
-
-            steps = [begin] + [nothing] * wait + [start, horner("a0", "a1", -ROOT / 4.0), horner("a1", "a0", ROOT / 3.0),
-                                                  horner("a0", "a1", -ROOT / 2.0), horner("a1", "a0", ROOT), end]
-            if lo == 0:
-                steps.append(negate)
-            return lambda: pending.extend(steps)
+            return [first, lambda: nc.scalar.activation(out=s("a1"), in_=s("x"), func=ACT.Ln),
+                    lambda: nc.vector.tensor_tensor(out=s("term"), in0=s("base"), in1=s("a1"), op=ALU.subtract)]
 
         def spread(i):
             def pe():
-                ps = [bank_s(), bank_s()]
+                ps = [bank(), bank()]
                 live[("cb", i)] = ps
                 for j in range(M_TILES):
                     nc.tensor.transpose(
@@ -365,23 +422,18 @@ def tile_lightgluematchabilityassignment_x2_kernel(
                         st[("term", i)][:, j : j + 1].to_broadcast([P, P]), ident[:],
                     )
 
-            def out():
-                ps = live[("cb", i)]
-                nc.scalar.copy(out=st[("cb", i)][:, 0:BANK], in_=ps[0][:])
-                nc.scalar.copy(out=st[("cb", i)][:, BANK:M], in_=ps[1][:, 0 : M - BANK])
-
-            return [pe, out]
+            return pe
 
         def result_tile(i, g, t):
             def add():
-                y = st[("y", i, g)]
+                y, ps = st[("y", i, g)], live[("cb", i)]
                 rows = out_0[i, g * BANK : (g + 1) * BANK, :].rearrange("(p t) m -> p t m", t=PACK)
                 k = M_TILES + PACK * g + t
-                nc.vector.scalar_tensor_tensor(
-                    out=y[:, t, :], in0=st[("cb", i)][:], scalar=st[("term", i)][:, k : k + 1], in1=y[:, t, :],
-                    op0=ALU.add, op1=ALU.subtract,
-                )
-                tick()
+                for src, part in ((ps[0][:], slice(0, BANK)), (ps[1][:, 0 : M - BANK], slice(BANK, M))):
+                    nc.vector.scalar_tensor_tensor(
+                        out=y[:, t, part], in0=src, scalar=st[("term", i)][:, k : k + 1], in1=y[:, t, part],
+                        op0=ALU.add, op1=ALU.subtract,
+                    )
                 nc.sync.dma_start(out=rows[:, t, :], in_=y[:, t, :])
 
             return [nothing, add]
@@ -427,19 +479,23 @@ def tile_lightgluematchabilityassignment_x2_kernel(
 
             def quant():
                 if ("yc", i, g) not in live:
-                    live[("left", i, g)] = [0, 1, 2]
                     live[("yc", i, g)] = rot.tile([P, M], U32, name="y_codes", align_bytes=64)
                 codes = live[("yc", i, g)]
                 quantize(codes[:, cols], y_scales[:, g, M * i + 256 * k : M * i + 256 * (k + 1)],
                          live[("yb", i, g, k)][:].rearrange("p m t -> p (m t)"))
-                live[("left", i, g)].remove(k)
-                if not live[("left", i, g)]:
-                    nc.sync.dma_start(
-                        out=out_1[g, :, M * i : M * (i + 1), :].rearrange("p m t -> p (m t)").bitcast(I32),
-                        in_=codes[:].bitcast(I32),
-                    )
+                nc.sync.dma_start(
+                    out=out_1[g, :, M * i + 256 * k : M * i + 256 * (k + 1), :].rearrange("p m t -> p (m t)").bitcast(I32),
+                    in_=codes[:, cols].bitcast(I32),
+                )
 
             return [nothing, pack, quant]
+
+        def both(f, g):
+            def go():
+                f()
+                g()
+
+            return go
 
         def run(slots):
             for k in range(-1, len(slots)):
@@ -450,118 +506,159 @@ def tile_lightgluematchabilityassignment_x2_kernel(
                     for pe, main in slots[k + 1]:
                         pe()
 
-        ROWNB = nc.vector
-
+        TURNED = []
+        QE = "PPGG"
         def keys(i):
             return [("a", i, 0, 0), ("a", i, 0, 1), ("a", i, 1, 0), ("a", i, 1, 1), ("b", i, 0), ("b", i, 1), ("b", i, 2)]
 
-        k0, k1 = keys(0), keys(1)
+        def item(unit, n, needs, gives):
+            return (both(unit[0], unit[1]) if n == 1 else unit[n], needs, gives)
 
-        def lead(unit):
-            return (unit[0], unit[1])
+        def T(k):
+            return item(turn(k), 1, [], [("T", k)])
 
-        def late(unit, n):
-            return (nothing, unit[n])
-
-        def only(thunk):
-            return (nothing, thunk)
-
-        def T(key):
-            return lead(turn(key))
-
-        def TQ(key):
-            return late(turn(key), 2)
+        def TQ(k):
+            return item(turn(k), 2, [("T", k)], [("TQ", k)])
 
         def PV(i, g, s):
-            return lead(project_tile(i, g, s))
-
-        def QQ(i, g, h):
-            return only(quant_q(i, g, h))
-
-        def A(i, g, h):
-            return lead(row_pair(i, g, h))
-
-        def J(i, g, h):
-            return late(row_pair(i, g, h), 2)
-
-        def BB(i, g, t):
-            return late(row_pair(i, g, t // 2), 3 + t % 2)
-
-        def CC(i, j, g):
-            return lead(column_half(i, j, g))
-
-        def DD(i, j):
-            return late(column_half(i, j, 1), 2)
+            return item(project_tile(i, g, s), 1, [("TQ", ("a", i, g, s // 2))], [])
 
         def PS(i, g, t):
-            return lead(project_slot(i, g, t))
+            return item(project_slot(i, g, t), 1, [("TQ", ("a", i, g, 0)), ("TQ", ("a", i, g, 1))], [("PS", i, g, t)])
 
-        def IL(i, g, h):
-            return only(interleave_q(i, g, h))
+        def IL(i, g, h, eng):
+            return (interleave_q(i, g, h, eng), [("PS", i, g, 3)], [("IL", i, g, h)])
 
-        def columns(i):
-            return [[CC(i, 0, 0)]] + [[CC(i, j + 1, 0), CC(i, j, 1)] for j in range(5)] + [[CC(i, 5, 1)]]
+        def QQ(i, g, h, needs=()):
+            return (quant_q(i, g, h), list(needs), [("QQ", i, g, h)])
 
-        def EV(i, g, t):
-            return lead(result_tile(i, g, t))
+        def A(i, g, h):
+            parts = row_pair(i, g, h)
+            return [(parts[n], [], [("A", i, g, h)] if n == 3 else []) for n in range(4)]
 
-        def ES(i, g, t):
-            return lead(result_turned(i, g, t))
+        def BB(i, g, t):
+            return (row_pair(i, g, t // 2)[4 + t % 2], [("A", i, g, t // 2)], [("B", i, g, t)])
+
+        def CC(i, j, g):
+            return item(column_half(i, j, g), 1, [], [("C", i, j, g)])
+
+        def DD(i, j):
+            return item(column_half(i, j, 1), 2, [("C", i, j, 1)], [("D", i, j)])
+
+        def cols(i):
+            out = [CC(i, 0, 0)]
+            for j in range(5):
+                out += [CC(i, j + 1, 0), CC(i, j, 1)]
+            return out + [CC(i, 5, 1)]
+
+        def EV(i, g, t, ev):
+            return item(result_tile(i, g, t), 1, [("cb", i), ("term", ev), ("B", i, g, t)], [("E", i, g, t)])
+
+        def ES(i, g, t, ev):
+            return item(result_turned(i, g, t), 1, [("nterm", i), ("term", ev), ("B", i, g, t)], [("E", i, g, t)])
 
         def F(i, g, k, eng):
-            return lead(plane_chunk(i, g, k, eng))
+            return item(plane_chunk(i, g, k, eng), 1, [("E", i, g, t) for t in range(4)], [("F", i, g, k)])
 
         def FQ(i, g, k):
-            return late(plane_chunk(i, g, k, "S"), 2)
+            return item(plane_chunk(i, g, k, "S"), 2, [("F", i, g, k)], [])
 
-        def put(slots, start, items, step=1):
-            for n, item in enumerate(items):
-                while len(slots) <= start + n * step:
-                    slots.append([])
-                slots[start + n * step].extend(item if isinstance(item, list) else [item])
+        def SP(i):
+            return (spread(i), [("nterm", i)], [("cb", i)])
 
-        def Z(key, e):
-            return (logits(key, e), nothing)
+        def Z(ks):
+            return [(logits(k, e), [("T", k)], [("Z", k, e)]) for k in ks for e in range(2)]
 
-        def ZZ(key):
-            return [Z(key, 0), Z(key, 1)]
+        def match(i, ks):
+            pick, fold, size, low, decay = matchability(i)
+            return ([(pick, [("Z", k, 1) for k in ks], []), (fold, [], [("fold", i)]), (low, [("size", i)], [])],
+                    [(size, [("fold", i)], [("size", i)]), (decay, [], [("ez", i)])])
 
-        slots = [
-            [T(k0[0])], [T(k0[1])], [T(k0[2]), TQ(k0[0])], [PV(0, 0, 0), TQ(k0[1]), PV(0, 0, 1), T(k0[3])],
-            [PV(0, 0, 2), QQ(0, 0, 0), TQ(k0[2]), PV(0, 0, 3), T(k0[4])],
-            [PV(0, 1, 0), TQ(k0[3]), QQ(0, 0, 1), PV(0, 1, 1), T(k0[5])],
-            [PV(0, 1, 2), TQ(k0[4]), QQ(0, 1, 0), PV(0, 1, 3), T(k0[6])],
-            [TQ(k0[5]), QQ(0, 1, 1), T(k1[0])],
-        ]
-        c0 = len(slots)
-        put(slots, c0, columns(0))
-        put(slots, c0, [[TQ(k0[6]), T(k1[1])], [TQ(k1[0]), T(k1[2])], [TQ(k1[1]), T(k1[3]), DD(0, 0)], [TQ(k1[2]), DD(0, 1)], [TQ(k1[3]), DD(0, 2)],
-                        [DD(0, 3), PS(1, 0, 0)], [DD(0, 4), PS(1, 0, 1)]])
-        put(slots, c0 + 2, [Z(key, e) for key in k0[4:] for e in range(2)][:5])
-        slots += [
-            [A(0, 0, 0), DD(0, 5), PS(1, 0, 2), PS(1, 0, 3), IL(1, 0, 0), IL(1, 0, 1), Z(k0[6], 1)] + ZZ(k0[0]),
-            [A(0, 0, 1), J(0, 0, 0), BB(0, 0, 0), BB(0, 0, 1), PS(1, 1, 0)] + ZZ(k0[1]),
-            [A(0, 1, 0), J(0, 0, 1)] + matchability(0, 0, 10) + [BB(0, 0, 2), BB(0, 0, 3), QQ(1, 0, 0), PS(1, 1, 1), PS(1, 1, 2), PS(1, 1, 3), only(terms(0, 0, 10, 3))] + ZZ(k0[2]),
-            [A(0, 1, 1), J(0, 1, 0), QQ(1, 0, 1), IL(1, 1, 0), IL(1, 1, 1), BB(0, 1, 0), BB(0, 1, 1), T(k1[4])] + ZZ(k0[3]),
-            [J(0, 1, 1)] + matchability(0, 10, 14) + [BB(0, 1, 2), BB(0, 1, 3), T(k1[5]), T(k1[6]), TQ(k1[4]), QQ(1, 1, 0), TQ(k1[5]), QQ(1, 1, 1), only(flush)],
-        ]
-        c1 = len(slots)
-        put(slots, c1, [[only(terms(0, 10, STATS, 2))], TQ(k1[6])])
-        put(slots, c1, columns(1))
-        put(slots, c1, [lead(spread(0)), ES(0, 0, 0), [ES(0, 0, 2), EV(0, 0, 1)], [DD(1, 0), EV(0, 0, 3)], [DD(1, 1), only(flush)], [DD(1, 2), ES(0, 1, 0)], [DD(1, 3), EV(0, 1, 1)]])
-        put(slots, c1 + 2, [Z(key, e) for key in k1[4:] for e in range(2)][:5])
-        slots += [
-            [A(1, 0, 0), DD(1, 4), DD(1, 5), Z(k1[6], 1)] + ZZ(k1[0]),
-            [A(1, 0, 1), J(1, 0, 0), BB(1, 0, 0), BB(1, 0, 1), ES(0, 1, 2), EV(0, 1, 3)] + ZZ(k1[1]),
-            [A(1, 1, 0), J(1, 0, 1)] + matchability(1, 0, 10) + [BB(1, 0, 2), BB(1, 0, 3), F(0, 0, 0, "S"), only(terms(1, 0, 10, 3))] + ZZ(k1[2]),
-            [A(1, 1, 1), J(1, 1, 0), BB(1, 1, 0), BB(1, 1, 1), FQ(0, 0, 0)] + ZZ(k1[3]),
-            [J(1, 1, 1)] + matchability(1, 10, 14) + [BB(1, 1, 2), BB(1, 1, 3), F(0, 0, 1, "S"), F(0, 0, 2, "S"), FQ(0, 0, 1), F(0, 1, 0, "S"), FQ(0, 0, 2), only(flush)],
-            [only(terms(1, 10, STATS, 2)), lead(spread(1)), F(0, 1, 1, "V"), FQ(0, 1, 0), F(0, 1, 2, "V"), FQ(0, 1, 1)],
-            [ES(1, 0, 0), EV(1, 0, 1), FQ(0, 1, 2)], [ES(1, 0, 2), EV(1, 0, 3), only(flush)],
-            [ES(1, 1, 0), EV(1, 1, 1), F(1, 0, 1, "V")], [ES(1, 1, 2), EV(1, 1, 3), F(1, 0, 2, "V"), F(1, 0, 0, "S"), FQ(1, 0, 1)],
-            [F(1, 1, 0, "S"), F(1, 1, 1, "V"), FQ(1, 0, 2), F(1, 1, 2, "V"), FQ(1, 0, 0)], [FQ(1, 1, 1), FQ(1, 1, 2), FQ(1, 1, 0)],
-        ]
-        run(slots)
+        def chain(i, lo, hi, ev, needs):
+            steps, exps = terms(i, lo, hi)
+            need = {0: needs + [("ez", i)], 3: [("e0", ev)], 8: [("e1", ev)]}
+            give = {1: [("g0", ev)], 6: [("g1", ev)], 13: [("term", ev)], 14: [("nterm", i)]}
+            return ([(f, need.get(n, []), give.get(n, [])) for n, f in enumerate(steps)],
+                    [(exps[0], [("g0", ev)], [("e0", ev)]), (exps[1], [("g1", ev)], [("e1", ev)])])
+
+        def chain_ln(i, lo, hi, ev, needs):
+            first, ln, end = terms_ln(i, lo, hi)
+            v = [(first, needs + [("ez", i)], [("g0", ev)]), (end, [("e0", ev)], [("term", ev)]), (terms(i, lo, hi)[0][14] if TURNED else nothing, [], [("nterm", i)])]
+            return v, [(ln, [("g0", ev)], [("e0", ev)]), (nothing, [], [])]
+
+        def weave(big, small, start=0, per=1):
+            out = []
+            for n, it in enumerate(big):
+                out.append(it)
+                if n >= start:
+                    out += small[(n - start) * per : (n - start + 1) * per]
+            return out + small[max(0, len(big) - start) * per :]
+
+        def run_lanes(lanes):
+            done = set()
+            at = [0] * len(lanes)
+            for turn_no in range(sum(len(lane) for lane in lanes)):
+                for n, lane in enumerate(lanes):
+                    if at[n] < len(lane) and all(need in done for need in lane[at[n]][1]):
+                        lane[at[n]][0]()
+                        done.update(lane[at[n]][2])
+                        at[n] += 1
+            assert at == [len(lane) for lane in lanes], at
+
+        k0, k1 = keys(0), keys(1)
+        def after(items, need):
+            return [(items[0][0], items[0][1] + [need], items[0][2])] + items[1:]
+
+        def EVs(i, g, ev):
+            return [EV(i, g, t, ev) for t in range(4) if t % 2 or (i, g, t // 2) not in TURNED]
+
+        def ESs(i, g, ev):
+            return [ES(i, g, t, ev) for t in range(4) if t % 2 == 0 and (i, g, t // 2) in TURNED]
+
+        m0v, m0s = match(0, k0)
+        m1v, m1s = match(1, k1)
+        c0v, c0s = chain(0, 0, STATS, 0, [("D", 0, 5), ("B", 0, 1, 3)])
+        c1v, c1s = chain_ln(1, 0, 10, 1, [("D", 1, 5), ("B", 1, 0, 3)])
+        last = terms_ln(1, 10, STATS)
+        FE = "SSSSSSSSVSVV"
+        fs = [F(n // 6, n // 3 % 2, n % 3, FE[n]) for n in range(12)]
+
+        def on(eng, lo, hi):
+            return [fs[n] for n in range(lo, hi) if FE[n] == eng]
+
+        def FQs(i, g):
+            n = 6 * i + 3 * g
+            return [FQ(i, g, k) for k in range(3) if FE[n + k] == "V"] + [FQ(i, g, k) for k in range(3) if FE[n + k] != "V"]
+
+        def qv(i, g):
+            if QE[2 * i + g] == "P":
+                return [PV(i, g, 0), PV(i, g, 1), PV(i, g, 2), QQ(i, g, 0), PV(i, g, 3), QQ(i, g, 1)]
+            return [QQ(i, g, h, [("IL", i, g, h)]) for h in range(2)]
+
+        def qs(i, g):
+            return [] if QE[2 * i + g] == "P" else [PS(i, g, t) for t in range(4)]
+
+        def qg(i, g):
+            return [] if QE[2 * i + g] == "P" else [IL(i, g, h, "G") for h in range(2)]
+
+        vector = [TQ(k0[0]), PV(0, 0, 0), TQ(k0[1]), PV(0, 0, 1), TQ(k0[4]), PV(0, 0, 2), QQ(0, 0, 0), TQ(k0[5]), PV(0, 0, 3), TQ(k0[6]),
+                  QQ(0, 0, 1)] + A(0, 0, 0) + [TQ(k0[2]), TQ(k0[3])] + A(0, 0, 1)
+        vector += weave(qv(0, 1), [TQ(k) for k in k1[0:4]]) + cols(0) + A(0, 1, 0) + [m0v[0]] + A(0, 1, 1)[0:2] + [m0v[1]] + A(0, 1, 1)[2:]
+        vector += weave(qv(1, 0) + qv(1, 1), [TQ(k) for k in k1[4:]])
+        vector += weave(cols(1) + A(1, 0, 0), [m0v[2]] + c0v, 0, 1) + [SP(0), m1v[0]]
+        vector += EVs(0, 0, 0) + [m1v[1]] + EVs(0, 1, 0) + A(1, 0, 1) + [m1v[2]] + A(1, 1, 0)[0:2]
+        vector += weave(A(1, 1, 0)[2:] + A(1, 1, 1) + on("V", 0, 6) + FQs(0, 0) + FQs(0, 1), c1v, 0, 1)
+        e10, e11 = EVs(1, 0, 1), EVs(1, 1, 2)
+        vector += [SP(1), (last[0], [("B", 1, 1, 3)], [("lx",)])] + e10 + [(last[2], [("ln",)], [("term", 2)])] + on("V", 6, 9) + e11 + FQs(1, 0) + on("V", 9, 12) + FQs(1, 1)
+        scalar = [T(k0[n]) for n in (0, 1, 4, 5, 6, 2, 3)] + qs(0, 1) + [T(k1[0]), BB(0, 0, 0), T(k1[1]), BB(0, 0, 1), T(k1[2]), T(k1[3])]
+        scalar += [BB(0, 0, 2), BB(0, 0, 3)] + weave([DD(0, j) for j in range(6)], qs(1, 0) + qs(1, 1) + [T(k) for k in k1[4:]], 0, 2)
+        scalar += [BB(0, 1, 0), BB(0, 1, 1), BB(0, 1, 2), BB(0, 1, 3), m0s[0], m0s[1], DD(1, 0), c0s[0], DD(1, 1), DD(1, 2), c0s[1], DD(1, 3), DD(1, 4), DD(1, 5)]
+        s0 = on("S", 0, 6)
+        scalar += [BB(1, 0, 0), BB(1, 0, 1)] + ESs(0, 0, 0) + ESs(0, 1, 0) + s0[0:1] + [m1s[0]] + s0[1:2] + [m1s[1]] + s0[2:3] + [BB(1, 0, 2), BB(1, 0, 3)]
+        scalar += [BB(1, 1, 0), c1s[0], BB(1, 1, 1)] + s0[3:4] + [c1s[1], BB(1, 1, 2), BB(1, 1, 3)] + s0[4:]
+        scalar += [(last[1], [("lx",)], [("ln",)])] + ESs(1, 0, 1) + ESs(1, 1, 2) + on("S", 6, 12)
+        others = qg(0, 1) + after(Z(k0), ("C", 0, 0, 0)) + qg(1, 0) + qg(1, 1) + after(Z(k1), ("C", 1, 0, 0)) + on("G", 0, 12)
+        run_lanes([vector, scalar, others])
         for quad in range(4):
             nc.sync.dma_start(
                 out=out_2[:, 4 * quad : 4 * quad + 4, :].rearrange("g r m -> r g m").bitcast(I32),

@@ -21,13 +21,17 @@ AXIS = mybir.AxisListType
 P = 128
 PACK = 4
 BANK = 512
-GROUPS = N // (P * PACK)
+QUADS = 4
+GROUPS = N // BANK
 M_TILES = M // P
+XB_PAIRS = M_TILES // 2
 STATS = M_TILES + GROUPS * PACK
-C = 1.0 / math.sqrt(D)
+M_PARTS = ((0, BANK), (BANK, M))
+CHUNK = 256
+SCALE = 1.0 / math.sqrt(D)
 HALF_CONST = 0.5 * (math.log(N) + math.log(M))
-LN2 = math.log(2.0)
-GUESS_SHIFT = 0.043
+GATHER_PAD = P - 32
+RAW_BUFS = 10
 
 
 def tile_lightgluematchabilityassignment_x2_kernel(
@@ -37,15 +41,15 @@ def tile_lightgluematchabilityassignment_x2_kernel(
     with ExitStack() as ctx:
         keep = ctx.enter_context(tc.tile_pool(name="keep", bufs=1))
         rot = ctx.enter_context(tc.tile_pool(name="rot", bufs=2))
-        psum = ctx.enter_context(tc.psum_pool(name="psum", bufs=4))
+        psum_v = ctx.enter_context(tc.psum_pool(name="psum_v", bufs=4))
         psum_s = ctx.enter_context(tc.psum_pool(name="psum_s", bufs=3))
         psum_z = ctx.enter_context(tc.psum_pool(name="psum_z", bufs=1))
 
         def kept(name, shape, dtype):
             return keep.tile(shape, dtype, name=name, align_bytes=64)
 
-        def bank():
-            return psum.tile([P, BANK], F32, name="bank")
+        def bank_v():
+            return psum_v.tile([P, BANK], F32, name="bank_v")
 
         def bank_s():
             return psum_s.tile([P, BANK], F32, name="bank_s")
@@ -55,53 +59,62 @@ def tile_lightgluematchabilityassignment_x2_kernel(
         w_codes = kept("w_codes", [P, 2 * D], U8)
         w_sc = kept("w_sc", [P, D], U8)
         ident = kept("ident", [P, P], F32)
+        gather = kept("gather", [P, GATHER_PAD + P], F32)
+        own_slot = kept("own_slot", [P, PACK], F32)
         b_sb = kept("b_sb", [P, PACK], BF16)
         wza_sb = kept("wza_sb", [P, PACK], BF16)
         wzb_sb = kept("wzb_sb", [P, PACK], BF16)
-        warm_in = kept("warm_in", [P, 1], F32)
-        warm_out = kept("warm_out", [P, 1], F32)
+        preload_in = kept("preload_in", [P, 1], F32)
+        preload_out = kept("preload_out", [P, 1], F32)
         y_scales = kept("y_scales", [P, GROUPS, B * M], U8)
+        z_bank = psum_z.tile([P, BANK], F32, name="z_bank")
 
         nc.vector.memset(ws_raw[:].bitcast(I32), 0)
-        nc.vector.memset(warm_in[:], 0.0)
-        nc.scalar.activation(out=warm_out[:], in_=warm_in[:], func=ACT.Exp)
-        gather = kept("gather", [P, 224], F32)
+        nc.vector.memset(preload_in[:], 0.0)
+        nc.scalar.activation(out=preload_out[:], in_=preload_in[:], func=ACT.Exp)
+
         with tc.manual_schedule(engines={mybir.EngineType.Pool}):
             make_identity(nc, ident[:])
             nc.gpsimd.dma_start(out=b_sb[:], in_=b.rearrange("(p t) -> p t", t=PACK))
             nc.gpsimd.memset(gather[:], 1.0)
-            nc.gpsimd.affine_select(out=gather[:], in_=gather[:], compare_op=ALU.is_ge, fill=0.0, base=4 * 96, pattern=[[-4, 224]], channel_multiplier=1)
-            nc.gpsimd.affine_select(out=gather[:], in_=gather[:], compare_op=ALU.is_ge, fill=0.0, base=3 - 4 * 96, pattern=[[4, 224]], channel_multiplier=-1)
+            nc.gpsimd.affine_select(
+                out=gather[:], in_=gather[:], compare_op=ALU.is_ge, fill=0.0,
+                base=PACK * GATHER_PAD, pattern=[[-PACK, GATHER_PAD + P]], channel_multiplier=1,
+            )
+            nc.gpsimd.affine_select(
+                out=gather[:], in_=gather[:], compare_op=ALU.is_ge, fill=0.0,
+                base=PACK - 1 - PACK * GATHER_PAD, pattern=[[PACK, GATHER_PAD + P]], channel_multiplier=-1,
+            )
             nc.gpsimd.dma_start(out=wza_sb[:], in_=wza.rearrange("(p t) -> p t", t=PACK))
             nc.gpsimd.dma_start(out=wzb_sb[:], in_=wzb.rearrange("(p t) -> p t", t=PACK))
 
         raw = {}
 
         def load_a(i, g, h):
-            raw[("a", i, g, h)] = kept("xa_%d%d%d" % (i, g, h), [P, 2, D], BF16)
-            rows = xa[i, g * BANK : (g + 1) * BANK, :].rearrange("(p t) d -> p t d", t=PACK)
-            nc.sync.dma_start(out=raw[("a", i, g, h)][:], in_=rows[:, 2 * h : 2 * h + 2, :])
+            raw["a", i, g, h] = rot.tile([P, 2, D], BF16, name="raw", bufs=RAW_BUFS)
+            points = xa[i, g * BANK : (g + 1) * BANK, :].rearrange("(p t) d -> p t d", t=PACK)
+            nc.sync.dma_start(out=raw["a", i, g, h][:], in_=points[:, 2 * h : 2 * h + 2, :])
 
         def load_b(i, h):
-            raw[("b", i, h)] = kept("xb_%d%d" % (i, h), [P, 2, D], BF16)
-            rows = xb[i, 2 * P * h : 2 * P * (h + 1), :].rearrange("(j p) d -> p j d", p=P)
-            nc.sync.dma_start(out=raw[("b", i, h)][:], in_=rows)
+            raw["b", i, 0, h] = rot.tile([P, 2, D], BF16, name="raw", bufs=RAW_BUFS)
+            points = xb[i, 2 * P * h : 2 * P * (h + 1), :].rearrange("(j p) d -> p j d", p=P)
+            nc.sync.dma_start(out=raw["b", i, 0, h][:], in_=points)
 
         with tc.manual_schedule(engines={mybir.EngineType.SP}):
             load_a(0, 0, 0)
             nc.sync.dma_start(out=w_raw[:].bitcast(I32), in_=w_words[0].bitcast(I32))
             load_a(0, 0, 1)
-            for quad in range(4):
+            for quad in range(QUADS):
                 nc.sync.dma_start(
                     out=ws_raw[32 * quad : 32 * quad + 4, :].bitcast(I32),
                     in_=w_scales[0, 4 * quad : 4 * quad + 4, :].bitcast(I32),
                 )
-            for h in range(3):
+            for h in range(XB_PAIRS):
                 load_b(0, h)
             for i, g in ((0, 1), (1, 0), (1, 1)):
                 for h in range(2):
                     load_a(i, g, h)
-            for h in range(3):
+            for h in range(XB_PAIRS):
                 load_b(1, h)
 
         nc.vector.tensor_copy(
@@ -112,554 +125,313 @@ def tile_lightgluematchabilityassignment_x2_kernel(
             out=w_sc[:].rearrange("p (t m) -> p t m", t=PACK),
             in_=ws_raw[:].rearrange("p (m t) -> p t m", t=PACK),
         )
-
-        pending = []
-
-        def tick():
-            if pending:
-                pending[0]()
-                pending.remove(pending[0])
+        nc.vector.tensor_reduce(
+            out=own_slot[:], in_=ident[:].rearrange("p (a t) -> p t a", t=PACK), axis=AXIS.X, op=ALU.add
+        )
 
         def quantize(codes, scales, grouped):
             nc.vector.quantize_mx(out=codes.bitcast(FP8X4), scales=scales, in_=grouped)
-            tick()
 
-        def mx(out, lhs, lhs_sc, rhs, rhs_sc, lhs_dtype=FP8X4):
+        def mx_scores(out, lhs, rhs, lhs_cols, rhs_cols):
+            with tc.high_priority():
+                nc.tensor.matmul_mx(
+                    out=out, lhsT=lhs[0][:, lhs_cols].bitcast(FP8X4), lhsT_scale=lhs[1][:, lhs_cols],
+                    rhs=rhs[0][:, rhs_cols].bitcast(FP8X4), rhs_scale=rhs[1][:, rhs_cols], start=True, stop=True,
+                )
+
+        def mx_project(out, t, rhs, rhs_cols):
             nc.tensor.matmul_mx(
-                out=out, lhsT=lhs.bitcast(lhs_dtype), lhsT_scale=lhs_sc,
-                rhs=rhs.bitcast(FP8X4), rhs_scale=rhs_sc, start=True, stop=True,
+                out=out, lhsT=w_codes[:, 2 * P * t : 2 * P * (t + 1)].bitcast(FP4X4),
+                lhsT_scale=w_sc[:, P * t : P * (t + 1)],
+                rhs=rhs[0][:, rhs_cols].bitcast(FP8X4), rhs_scale=rhs[1][:, rhs_cols], start=True, stop=True,
             )
 
-        st = {}
-        for i in range(B):
-            for name in ("nbr", "sum", "x", "ny0", "ny1", "ex", "u", "r", "a0", "a1", "absz", "ez", "mz", "base", "term", "nterm"):
-                st[(name, i)] = kept("%s_%d" % (name, i), [P, STATS], F32)
-            st[("half", i)] = kept("half_%d" % i, [P, STATS, 2], F32)
-            st[("xb_c", i)] = kept("xb_c%d" % i, [P, M], U32)
-            st[("xb_s", i)] = kept("xb_s%d" % i, [P, M], U8)
-            for g in range(GROUPS):
-                for name in ("xa", "q"):
-                    st[(name + "_c", i, g)] = kept("%s_c%d%d" % (name, i, g), [P, BANK], U32)
-                    st[(name + "_s", i, g)] = kept("%s_s%d%d" % (name, i, g), [P, BANK], U8)
-                st[("y", i, g)] = kept("y%d%d" % (i, g), [P, PACK, M], F32)
-        own_slot = kept("own_slot", [P, PACK], F32)
-        nc.vector.tensor_reduce(out=own_slot[:], in_=ident[:].rearrange("p (a t) -> p t a", t=PACK), axis=AXIS.X, op=ALU.add)
-        live = {}
-        z_bank = psum_z.tile([P, BANK], F32, name="z")
+        def operand(name, width):
+            return (kept(name + "_codes", [P, width], U32), kept(name + "_scales", [P, width], U8))
 
-        def flush():
-            for k in range(len(pending)):
-                tick()
+        xa_mx = {(i, g): operand("xa%d%d" % (i, g), BANK) for i in range(B) for g in range(GROUPS)}
+        q_mx = {(i, g): operand("q%d%d" % (i, g), BANK) for i in range(B) for g in range(GROUPS)}
+        xb_mx = {i: operand("xb%d" % i, M) for i in range(B)}
+        y = {(i, g): kept("y%d%d" % (i, g), [P, PACK, M], F32) for i in range(B) for g in range(GROUPS)}
+        stat = {
+            (name, i): kept("%s%d" % (name, i), [P, STATS], F32)
+            for name in ("first", "low", "shift", "total", "absz", "ez", "mz", "x", "base", "ln", "term", "nterm")
+            for i in range(B)
+        }
+        turned = {}
+        col_scores = {}
+        col_term = {}
 
-        def nothing():
-            return None
+        def on_scalar(t):
+            return t % 2 == 0
 
-        def turn(key):
-            cols = slice(2 * P * key[-1], 2 * P * (key[-1] + 1))
-            dst = ("xa_c",) + key[1:3] if key[0] == "a" else ("xb_c", key[1])
-            dst_s = ("xa_s",) + key[1:3] if key[0] == "a" else ("xb_s", key[1])
-
-            def pe():
-                words = raw[key][:].rearrange("p a d -> p (a d)").bitcast(F32)
+        def turn(kind, i, g, pairs):
+            tile = kept("turned_%s%d%d%d" % (kind, i, g, pairs[0]), [P, 2 * BANK * len(pairs)], BF16)
+            for n, h in enumerate(pairs):
+                words = raw[kind, i, g, h][:].rearrange("p a d -> p (a d)").bitcast(F32)
                 ps = bank_s()
-                live[key] = ps
                 for a in range(2):
                     for u in range(2):
                         k = 2 * a + u
                         nc.tensor.transpose(
-                            ps[:, P * k : P * (k + 1)], words[:, 256 * a + u : 256 * (a + 1) : 2], ident[:]
+                            ps[:, P * k : P * (k + 1)], words[:, D // 2 * a + u : D // 2 * (a + 1) : 2], ident[:]
                         )
-
-            def out():
-                xt = kept("xt_" + "".join(str(s) for s in key), [P, 2 * P * PACK], BF16)
-                live[("xt",) + key] = xt
+                turned[kind, i, g, h] = tile[:, 2 * BANK * n : 2 * BANK * (n + 1)]
                 nc.scalar.copy(
-                    out=xt[:].bitcast(F32).rearrange("p (a r u) -> p a r u", a=2, u=2),
-                    in_=live[key][:].rearrange("p (a u r) -> p a r u", a=2, u=2),
+                    out=turned[kind, i, g, h].bitcast(F32).rearrange("p (a r u) -> p a r u", a=2, u=2),
+                    in_=ps[:].rearrange("p (a u r) -> p a r u", a=2, u=2),
                 )
+            codes, scales = xa_mx[i, g] if kind == "a" else xb_mx[i]
+            cols = slice(2 * P * pairs[0], 2 * P * (pairs[-1] + 1))
+            quantize(codes[:, cols], scales[:, cols], tile[:])
 
-            def quant():
-                quantize(st[dst][:, cols], st[dst_s][:, cols], live[("xt",) + key][:])
+        def turn_b(i):
+            turn("b", i, 0, [0, 1])
+            turn("b", i, 0, [2])
 
-            return [pe, out, quant]
-
-        def logits(key, a):
-            i = key[1]
-            k = M_TILES + PACK * key[2] + 2 * key[3] + a if key[0] == "a" else 2 * key[2] + a
-            wz = wza_sb if key[0] == "a" else wzb_sb
-
-            def pe():
-                for q in range(4):
-                    col = PACK * (STATS * (4 * i + q) + k)
-                    lo = BANK * a + P * q
-                    nc.tensor.matmul(z_bank[:, col : col + PACK], lhsT=live[("xt",) + key][:, lo : lo + P], rhs=wz[:],
-                                     start=True, stop=True)
-
-            return pe
-
-        def project_tile(i, g, s):
-            cols = slice(P * s, P * (s + 1))
-            h, a = divmod(s, 2)
-
-            def pe():
-                ps = bank()
-                live[("p", i, g, s)] = ps
-                with tc.high_priority():
-                    for t in range(PACK):
-                        mx(ps[:, P * t : P * (t + 1)], w_codes[:, 2 * P * t : 2 * P * (t + 1)],
-                           w_sc[:, P * t : P * (t + 1)], st[("xa_c", i, g)][:, cols], st[("xa_s", i, g)][:, cols], FP4X4)
-
-            def out():
-                if a == 0:
-                    live[("qg", i, g, h)] = rot.tile([P, 2 * P, PACK], BF16, name="qg", bufs=4, align_bytes=64)
-                nc.vector.tensor_tensor(
-                    out=live[("qg", i, g, h)][:, P * a : P * (a + 1), :],
-                    in0=live[("p", i, g, s)][:].rearrange("p (t n) -> p n t", t=PACK),
-                    in1=b_sb[:].unsqueeze(1).to_broadcast([P, P, PACK]),
-                    op=ALU.add,
-                )
-
-            return [pe, out, quant_q(i, g, h) if a == 1 else nothing]
-
-        def quant_q(i, g, h):
-            def quant():
-                cols = slice(2 * P * h, 2 * P * (h + 1))
-                quantize(st[("q_c", i, g)][:, cols], st[("q_s", i, g)][:, cols],
-                         live[("qg", i, g, h)][:].rearrange("p n t -> p (n t)"))
-
-            return quant
-
-        def project_slot(i, g, t):
-            def pe():
-                ps = bank_s()
-                live[("p", i, g, t)] = ps
-                mx(ps[:], w_codes[:, 2 * P * t : 2 * P * (t + 1)], w_sc[:, P * t : P * (t + 1)],
-                   st[("xa_c", i, g)][:], st[("xa_s", i, g)][:], FP4X4)
-
-            def out():
-                if t == 0:
-                    live[("qs", i, g)] = rot.tile([P, PACK, BANK], BF16, name="qs", bufs=2, align_bytes=64)
-                nc.scalar.activation(out=live[("qs", i, g)][:, t, :], in_=live[("p", i, g, t)][:],
-                                     func=ACT.Identity, bias=b_sb[:, t : t + 1])
-
-            return [pe, out, nothing]
-
-        def interleave_q(i, g, h, eng):
-            def go():
-                cols = slice(2 * P * h, 2 * P * (h + 1))
-                live[("qg", i, g, h)] = rot.tile([P, 2 * P, PACK], BF16, name="qg", bufs=4, align_bytes=64)
-                if eng == "G":
-                    nc.gpsimd.tensor_scalar(
-                        out=live[("qg", i, g, h)][:], in0=live[("qs", i, g)][:, :, cols].rearrange("p t n -> p n t"),
-                        scalar1=1.0, scalar2=0.0, op0=ALU.mult, op1=ALU.add,
-                    )
-                else:
-                    nc.vector.tensor_copy(
-                        out=live[("qg", i, g, h)][:].rearrange("p (c e) t -> p c t e", e=4),
-                        in_=live[("qs", i, g)][:, :, cols].rearrange("p t (c e) -> p c t e", e=4),
-                    )
-                    tick()
-
-            return go
-
-        def matchability(i):
-            n = 4 * STATS
-            zm = kept("zm%d" % i, [P, n, PACK], F32)
-            zz = kept("zz%d" % i, [P, n], F32)
-            z = z_bank[:, B * PACK * n + STATS * i : B * PACK * n + STATS * (i + 1)]
-            absz, ez, mz = st[("absz", i)], st[("ez", i)], st[("mz", i)]
-
-            def pick():
-                nc.vector.tensor_tensor(
-                    out=zm[:], in0=z_bank[:, PACK * n * i : PACK * n * (i + 1)].rearrange("p (c t) -> p c t", t=PACK),
-                    in1=own_slot[:].unsqueeze(1).to_broadcast([P, n, PACK]), op=ALU.mult,
-                )
-
-            def fold():
-                nc.vector.tensor_reduce(out=zz[:], in_=zm[:], axis=AXIS.X, op=ALU.add)
-                for q in range(4):
-                    nc.tensor.matmul(z, lhsT=gather[:, 96 - 32 * q : 224 - 32 * q], rhs=zz[:, STATS * q : STATS * (q + 1)],
-                                     start=(q == 0), stop=(q == 3))
-
-            def size():
-                nc.scalar.activation(out=absz[:], in_=z, func=ACT.Abs)
-
-            def low():
-                nc.vector.tensor_scalar(out=mz[:], in0=z, scalar1=0.0, scalar2=HALF_CONST, op0=ALU.min, op1=ALU.add)
-
-            def decay():
-                nc.scalar.activation(out=ez[:], in_=absz[:], func=ACT.Exp, scale=-1.0)
-
-            return [pick, fold, size, low, decay]
-
-        def scores(src, dst, scale, first, acc):
-            nc.vector.tensor_scalar(out=dst, in0=src, scalar1=scale, scalar2=first, op0=ALU.mult, op1=ALU.min, accum_out=acc)
-            tick()
-
-        def row_pair(i, g, h):
-            turned = (i, g, h) in TURNED
-            s0 = -C if turned else -2.0 * C
-            y, half, nb = st[("y", i, g)], st[("half", i)], st[("nbr", i)]
-            t0, t1 = 2 * h, 2 * h + 1
-            k0, k1 = M_TILES + PACK * g + t0, M_TILES + PACK * g + t1
-
-            def part(t, k, lo, hi, scale, first, acc):
-                def go():
-                    ps = bank()
-                    cols = slice(P * t, P * (t + 1))
+        def project_on_vector(i, g):
+            for h in range(2):
+                q_pair = rot.tile([P, 2 * P, PACK], BF16, name="q_pair", align_bytes=64)
+                for a in range(2):
+                    ps = bank_v()
+                    points = slice(P * (2 * h + a), P * (2 * h + a + 1))
                     with tc.high_priority():
-                        mx(ps[:, 0 : hi - lo], st[("q_c", i, g)][:, cols], st[("q_s", i, g)][:, cols],
-                           st[("xb_c", i)][:, lo:hi], st[("xb_s", i)][:, lo:hi])
-                    scores(ps[:, 0 : hi - lo], y[:, t, lo:hi], scale, first, acc)
-
-                return go
-
-            def join():
-                lo = k1 if turned else k0
-                nc.scalar.activation(out=nb[:, lo : k1 + 1], in_=half[:, lo : k1 + 1, 1], func=ACT.Copy, scale=0.5)
-
-            def total(t, k, scale):
-                def go():
-                    junk = rot.tile([P, N], BF16, name="junk", bufs=3)
-                    nc.scalar.activation(
-                        out=junk[:, 0:M], in_=y[:, t, :], func=ACT.Exp, scale=scale, bias=nb[:, k : k + 1],
-                        accum_out=st[("sum", i)][:, k : k + 1],
+                        for t in range(PACK):
+                            mx_project(ps[:, P * t : P * (t + 1)], t, xa_mx[i, g], points)
+                    nc.vector.tensor_tensor(
+                        out=q_pair[:, P * a : P * (a + 1), :], in0=ps[:].rearrange("p (t n) -> p n t", t=PACK),
+                        in1=b_sb[:].unsqueeze(1).to_broadcast([P, P, PACK]), op=ALU.add,
                     )
+                cols = slice(2 * P * h, 2 * P * (h + 1))
+                quantize(q_mx[i, g][0][:, cols], q_mx[i, g][1][:, cols], q_pair[:].rearrange("p n t -> p (n t)"))
 
-                return go
+        def project_beside_vector(i, g):
+            q_slices = rot.tile([P, PACK, BANK], BF16, name="q_slices", align_bytes=64)
+            for t in range(PACK):
+                ps = bank_s()
+                mx_project(ps[:], t, xa_mx[i, g], slice(0, BANK))
+                nc.scalar.activation(out=q_slices[:, t, :], in_=ps[:], func=ACT.Identity, bias=b_sb[:, t : t + 1])
+            q_group = rot.tile([P, BANK, PACK], BF16, name="q_group", align_bytes=64)
+            for h in range(2):
+                cols = slice(2 * P * h, 2 * P * (h + 1))
+                nc.gpsimd.tensor_scalar(
+                    out=q_group[:, cols, :], in0=q_slices[:, :, cols].rearrange("p t n -> p n t"),
+                    scalar1=1.0, scalar2=0.0, op0=ALU.mult, op1=ALU.add,
+                )
+            quantize(q_mx[i, g][0][:], q_mx[i, g][1][:], q_group[:].rearrange("p n t -> p (n t)"))
 
-            return [part(t0, k0, 0, BANK, s0, None, half[:, k0, 0:1]), part(t1, k1, 0, BANK, -2.0 * C, None, half[:, k1, 0:1]),
-                    part(t0, k0, BANK, M, s0, half[:, k0, 0:1], nb[:, k0 : k0 + 1] if turned else half[:, k0, 1:2]),
-                    part(t1, k1, BANK, M, -2.0 * C, half[:, k1, 0:1], half[:, k1, 1:2]),
-                    both(join, total(t0, k0, -1.0 if turned else -0.5)), total(t1, k1, -0.5)]
+        def logits(i):
+            tiles = [("b", 0, h, a, 2 * h + a) for h in range(XB_PAIRS) for a in range(2)]
+            tiles += [
+                ("a", g, h, a, M_TILES + PACK * g + 2 * h + a) for g in range(GROUPS) for h in range(2) for a in range(2)
+            ]
+            for kind, g, h, a, k in tiles:
+                for q in range(QUADS):
+                    col = PACK * (STATS * (QUADS * i + q) + k)
+                    lo = BANK * a + P * q
+                    nc.tensor.matmul(
+                        z_bank[:, col : col + PACK], lhsT=turned[kind, i, g, h][:, lo : lo + P],
+                        rhs=(wza_sb if kind == "a" else wzb_sb)[:], start=True, stop=True,
+                    )
+            n = QUADS * STATS
+            picked = kept("picked%d" % i, [P, n, PACK], F32)
+            folded = kept("folded%d" % i, [P, n], F32)
+            z = z_bank[:, B * PACK * n + STATS * i : B * PACK * n + STATS * (i + 1)]
+            nc.vector.tensor_tensor(
+                out=picked[:], in0=z_bank[:, PACK * n * i : PACK * n * (i + 1)].rearrange("p (c t) -> p c t", t=PACK),
+                in1=own_slot[:].unsqueeze(1).to_broadcast([P, n, PACK]), op=ALU.mult,
+            )
+            nc.vector.tensor_reduce(out=folded[:], in_=picked[:], axis=AXIS.X, op=ALU.add)
+            for q in range(QUADS):
+                nc.tensor.matmul(
+                    z, lhsT=gather[:, GATHER_PAD - 32 * q : GATHER_PAD - 32 * q + P],
+                    rhs=folded[:, STATS * q : STATS * (q + 1)], start=(q == 0), stop=(q == QUADS - 1),
+                )
+            nc.scalar.activation(out=stat["absz", i][:], in_=z, func=ACT.Abs)
+            nc.vector.tensor_scalar(
+                out=stat["mz", i][:], in0=z, scalar1=0.0, scalar2=HALF_CONST, op0=ALU.min, op1=ALU.add
+            )
+            nc.scalar.activation(out=stat["ez", i][:], in_=stat["absz", i][:], func=ACT.Exp, scale=-1.0)
+
+        def empty_scores(src, dst, factor, first, least):
+            nc.vector.tensor_scalar(
+                out=dst, in0=src, scalar1=factor, scalar2=first, op0=ALU.mult, op1=ALU.min, accum_out=least
+            )
+
+        def exp_sum(i, k, src, factor):
+            exps = rot.tile([P, N], BF16, name="exps", bufs=3)
+            nc.scalar.activation(
+                out=exps[:, 0 : src.shape[1]], in_=src, func=ACT.Exp, scale=factor,
+                bias=stat["shift", i][:, k : k + 1], accum_out=stat["total", i][:, k : k + 1],
+            )
+
+        def rows(i, g, h):
+            slots = (2 * h, 2 * h + 1)
+            k0 = M_TILES + PACK * g
+            for lo, hi in M_PARTS:
+                for t in slots:
+                    k = k0 + t
+                    ps = bank_v()
+                    mx_scores(ps[:, 0 : hi - lo], q_mx[i, g], xb_mx[i], slice(P * t, P * (t + 1)), slice(lo, hi))
+                    first = stat["first", i][:, k : k + 1]
+                    last = stat["shift" if on_scalar(t) else "low", i][:, k : k + 1]
+                    empty_scores(
+                        ps[:, 0 : hi - lo], y[i, g][:, t, lo:hi], -SCALE if on_scalar(t) else -2.0 * SCALE,
+                        first if lo else None, last if lo else first,
+                    )
+            odd = slice(k0 + slots[1], k0 + slots[1] + 1)
+            nc.scalar.activation(out=stat["shift", i][:, odd], in_=stat["low", i][:, odd], func=ACT.Copy, scale=0.5)
+            for t in slots:
+                exp_sum(i, k0 + t, y[i, g][:, t, :], -1.0 if on_scalar(t) else -0.5)
 
         def column_half(i, j, g):
-            half, nb = st[("half", i)], st[("nbr", i)]
-            cols = slice(P * j, P * (j + 1))
+            if g == 0:
+                col_scores[i, j] = rot.tile([P, N], F32, name="col_scores", bufs=B * M_TILES)
+            ps = bank_v()
+            mx_scores(ps[:], xb_mx[i], q_mx[i, g], slice(P * j, P * (j + 1)), slice(0, BANK))
+            first = stat["first", i][:, j : j + 1]
+            empty_scores(
+                ps[:], col_scores[i, j][:, BANK * g : BANK * (g + 1)], -SCALE,
+                first if g else None, stat["shift", i][:, j : j + 1] if g else first,
+            )
+            if g == 1:
+                exp_sum(i, j, col_scores[i, j][:], -1.0)
 
-            def pe():
-                ps = bank()
-                live[("c", i, j, g)] = ps
-                with tc.high_priority():
-                    mx(ps[:], st[("xb_c", i)][:, cols], st[("xb_s", i)][:, cols], st[("q_c", i, g)][:], st[("q_s", i, g)][:])
-
-            def peak():
-                if g == 0:
-                    live[("st", i, j)] = rot.tile([P, N], F32, name="s_t", bufs=12 if TURNED else 5)
-                scores(live[("c", i, j, g)][:], live[("st", i, j)][:, BANK * g : BANK * (g + 1)], -C,
-                       half[:, j, 0:1] if g else None, nb[:, j : j + 1] if g else half[:, j, 0:1])
-
-            def total():
-                junk = rot.tile([P, N], BF16, name="junk", bufs=3)
-                nc.scalar.activation(
-                    out=junk[:], in_=live[("st", i, j)][:], func=ACT.Exp, scale=-1.0, bias=nb[:, j : j + 1],
-                    accum_out=st[("sum", i)][:, j : j + 1],
-                )
-
-            return [pe, peak, total]
+        def columns(i):
+            column_half(i, 0, 0)
+            for j in range(1, M_TILES):
+                column_half(i, j, 0)
+                column_half(i, j - 1, 1)
+            column_half(i, M_TILES - 1, 1)
 
         def terms(i, lo, hi):
-            def s(name):
-                return st[(name, i)][:, lo:hi]
-
-            def two(dst, a, z, op):
-                return lambda: nc.vector.tensor_tensor(out=s(dst), in0=s(a), in1=s(z), op=op)
-
-            def affine(dst, src, first, second, op0, op1):
-                return lambda: nc.vector.tensor_scalar(out=s(dst), in0=s(src), scalar1=first, scalar2=second, op0=op0, op1=op1)
-
-            def horner(dst, src, coef, other):
-                return lambda: nc.vector.scalar_tensor_tensor(out=s(dst), in0=s(src), scalar=coef, in1=s(other), op0=ALU.add, op1=ALU.mult)
-
-            def exp_of(src):
-                return lambda: nc.scalar.activation(out=s("ex"), in_=s(src), func=ACT.Exp)
-
-            def guess():
+            s = {name: stat[name, i][:, lo:hi] for name in ("x", "ez", "total", "ln", "base", "shift", "mz", "term")}
+            nc.vector.scalar_tensor_tensor(
+                out=s["x"], in0=s["ez"], scalar=1.0, in1=s["total"], op0=ALU.add, op1=ALU.mult
+            )
+            nc.scalar.activation(out=s["ln"], in_=s["x"], func=ACT.Ln)
+            nc.vector.tensor_tensor(out=s["base"], in0=s["shift"], in1=s["mz"], op=ALU.add)
+            nc.vector.tensor_tensor(out=s["term"], in0=s["base"], in1=s["ln"], op=ALU.subtract)
+            if lo == 0:
                 nc.vector.tensor_scalar(
-                    out=s("ny0"), in0=s("x").bitcast(I32), scalar1=-LN2 / 2.0**23, scalar2=(127.0 - GUESS_SHIFT) * LN2,
-                    op0=ALU.mult, op1=ALU.add,
+                    out=stat["nterm", i][:, 0:M_TILES], in0=stat["term", i][:, 0:M_TILES],
+                    scalar1=-0.5, scalar2=None, op0=ALU.mult,
                 )
 
-            steps = [
-                horner("x", "ez", 1.0, "sum"),
-                guess,
-                two("base", "nbr", "mz", ALU.add),
-                two("u", "x", "ex", ALU.mult),
-                affine("a0", "u", -0.5, 1.5, ALU.mult, ALU.add),
-                horner("a1", "u", -1.0, "a0"),
-                two("ny1", "ny0", "a1", ALU.subtract),
-                two("base", "base", "ny1", ALU.add),
-                two("u", "x", "ex", ALU.mult),
-                both(affine("r", "u", 1.0, -1.0, ALU.mult, ALU.add), affine("a0", "u", -1.0, -0.25, ALU.add, ALU.mult)),
-                horner("a1", "a0", 1.0 / 3.0, "r"),
-                horner("a0", "a1", -0.5, "r"),
-                horner("a1", "a0", 1.0, "r"),
-                two("term", "base", "a1", ALU.subtract),
-            ]
-            if lo == 0:
-                steps.append(lambda: nc.vector.tensor_scalar(out=st[("nterm", i)][:, 0:M_TILES], in0=st[("term", i)][:, 0:M_TILES],
-                                                             scalar1=-0.5, scalar2=None, op0=ALU.mult))
-            return steps, [exp_of("ny0"), exp_of("ny1")]
-
-        def terms_ln(i, lo, hi):
-            def s(name):
-                return st[(name, i)][:, lo:hi]
-
-            def first():
-                nc.vector.scalar_tensor_tensor(out=s("x"), in0=s("ez"), scalar=1.0, in1=s("sum"), op0=ALU.add, op1=ALU.mult)
-                nc.vector.tensor_tensor(out=s("base"), in0=s("nbr"), in1=s("mz"), op=ALU.add)
-
-            return [first, lambda: nc.scalar.activation(out=s("a1"), in_=s("x"), func=ACT.Ln),
-                    lambda: nc.vector.tensor_tensor(out=s("term"), in0=s("base"), in1=s("a1"), op=ALU.subtract)]
-
         def spread(i):
-            def pe():
-                ps = [bank(), bank()]
-                live[("cb", i)] = ps
+            ps = [bank_v(), bank_v()]
+            with tc.high_priority():
                 for j in range(M_TILES):
                     nc.tensor.transpose(
                         ps[j // 4][:, P * (j % 4) : P * (j % 4 + 1)],
-                        st[("term", i)][:, j : j + 1].to_broadcast([P, P]), ident[:],
+                        stat["term", i][:, j : j + 1].to_broadcast([P, P]), ident[:],
                     )
+            col_term[i] = ps
 
-            return pe
-
-        def result_tile(i, g, t):
-            def add():
-                y, ps = st[("y", i, g)], live[("cb", i)]
-                rows = out_0[i, g * BANK : (g + 1) * BANK, :].rearrange("(p t) m -> p t m", t=PACK)
+        def results(i, g):
+            out_rows = out_0[i, g * BANK : (g + 1) * BANK, :].rearrange("(p t) m -> p t m", t=PACK)
+            for t in range(PACK):
                 k = M_TILES + PACK * g + t
-                for src, part in ((ps[0][:], slice(0, BANK)), (ps[1][:, 0 : M - BANK], slice(BANK, M))):
-                    nc.vector.scalar_tensor_tensor(
-                        out=y[:, t, part], in0=src, scalar=st[("term", i)][:, k : k + 1], in1=y[:, t, part],
-                        op0=ALU.add, op1=ALU.subtract,
-                    )
-                nc.sync.dma_start(out=rows[:, t, :], in_=y[:, t, :])
-
-            return [nothing, add]
-
-        def result_turned(i, g, t):
-            k = M_TILES + PACK * g + t
-            cols = slice(BANK * g + P * t, BANK * g + P * (t + 1))
-
-            def pe():
-                ps = [bank_s(), bank_s()]
-                live[("e", i, g, t)] = ps
-                for j in range(M_TILES):
-                    dst = ps[j // 4][:, P * (j % 4) : P * (j % 4 + 1)]
-                    nc.tensor.matmul(dst, lhsT=live[("st", i, j)][:, cols], rhs=ident[:], is_transpose=True, start=True, stop=False)
-                    nc.tensor.matmul(dst, lhsT=st[("nterm", i)][:, j : j + 1].to_broadcast([P, P]), rhs=ident[:],
-                                     is_transpose=True, start=False, stop=True)
-
-            def add():
-                y, ps = st[("y", i, g)], live[("e", i, g, t)]
-                rows = out_0[i, g * BANK : (g + 1) * BANK, :].rearrange("(p t) m -> p t m", t=PACK)
-                for src, part in ((ps[0][:], slice(0, BANK)), (ps[1][:, 0 : M - BANK], slice(BANK, M))):
-                    nc.scalar.activation(out=y[:, t, part], in_=src, func=ACT.Identity, scale=-2.0, bias=st[("term", i)][:, k : k + 1])
-                nc.sync.dma_start(out=rows[:, t, :], in_=y[:, t, :])
-
-            return [pe, add]
-
-        def plane_chunk(i, g, k, eng):
-            cols = slice(256 * k, 256 * (k + 1))
-
-            def pack():
-                yb = rot.tile([P, 256, PACK], BF16, name="yb", bufs=6, align_bytes=64)
-                live[("yb", i, g, k)] = yb
-                dst = yb[:].rearrange("p (c e) t -> p c t e", e=4)
-                src = st[("y", i, g)][:, :, cols].rearrange("p t (c e) -> p c t e", e=4)
-                if eng == "S":
-                    nc.scalar.copy(out=dst, in_=src)
-                elif eng == "V":
-                    nc.vector.tensor_copy(out=dst, in_=src)
-                    tick()
+                row_term = stat["term", i][:, k : k + 1]
+                if on_scalar(t):
+                    points = slice(BANK * g + P * t, BANK * g + P * (t + 1))
+                    ps = [bank_s(), bank_s()]
+                    for j in range(M_TILES):
+                        dst = ps[j // 4][:, P * (j % 4) : P * (j % 4 + 1)]
+                        nc.tensor.matmul(
+                            dst, lhsT=col_scores[i, j][:, points], rhs=ident[:],
+                            is_transpose=True, start=True, stop=False,
+                        )
+                        nc.tensor.matmul(
+                            dst, lhsT=stat["nterm", i][:, j : j + 1].to_broadcast([P, P]), rhs=ident[:],
+                            is_transpose=True, start=False, stop=True,
+                        )
+                    for n, (lo, hi) in enumerate(M_PARTS):
+                        nc.scalar.activation(
+                            out=y[i, g][:, t, lo:hi], in_=ps[n][:, 0 : hi - lo], func=ACT.Identity,
+                            scale=-2.0, bias=row_term,
+                        )
                 else:
-                    nc.gpsimd.tensor_scalar(out=yb[:], in0=st[("y", i, g)][:, :, cols].rearrange("p t m -> p m t"),
-                                            scalar1=1.0, scalar2=0.0, op0=ALU.mult, op1=ALU.add)
+                    for n, (lo, hi) in enumerate(M_PARTS):
+                        nc.vector.scalar_tensor_tensor(
+                            out=y[i, g][:, t, lo:hi], in0=col_term[i][n][:, 0 : hi - lo], scalar=row_term,
+                            in1=y[i, g][:, t, lo:hi], op0=ALU.add, op1=ALU.subtract,
+                        )
+                nc.sync.dma_start(out=out_rows[:, t, :], in_=y[i, g][:, t, :])
 
-            def quant():
-                if ("yc", i, g) not in live:
-                    live[("yc", i, g)] = rot.tile([P, M], U32, name="y_codes", align_bytes=64)
-                codes = live[("yc", i, g)]
-                quantize(codes[:, cols], y_scales[:, g, M * i + 256 * k : M * i + 256 * (k + 1)],
-                         live[("yb", i, g, k)][:].rearrange("p m t -> p (m t)"))
-                nc.sync.dma_start(
-                    out=out_1[g, :, M * i + 256 * k : M * i + 256 * (k + 1), :].rearrange("p m t -> p (m t)").bitcast(I32),
-                    in_=codes[:, cols].bitcast(I32),
+        def pack_on_gpsimd(dst, src):
+            nc.gpsimd.tensor_scalar(
+                out=dst.rearrange("p (m t) -> p m t", t=PACK), in0=src.rearrange("p t m -> p m t"),
+                scalar1=1.0, scalar2=0.0, op0=ALU.mult, op1=ALU.add,
+            )
+
+        def pack_with(copy):
+            def pack(dst, src):
+                copy(
+                    out=dst.rearrange("p (c e t) -> p c t e", e=4, t=PACK),
+                    in_=src.rearrange("p t (c e) -> p c t e", e=4),
                 )
 
-            return [nothing, pack, quant]
+            return pack
 
-        def both(f, g):
-            def go():
-                f()
-                g()
+        pack_on_scalar = pack_with(nc.scalar.copy)
+        pack_on_vector = pack_with(nc.vector.tensor_copy)
 
-            return go
+        def planes(i, g, packers, parts):
+            codes = rot.tile([P, M], U32, name="y_codes", align_bytes=64)
+            for lo, hi in parts:
+                y_bf16 = rot.tile([P, BANK * PACK], BF16, name="y_bf16", bufs=3, align_bytes=64)
+                for c in range(lo, hi, CHUNK):
+                    packers[c // CHUNK](
+                        y_bf16[:, PACK * (c - lo) : PACK * (c - lo + CHUNK)], y[i, g][:, :, c : c + CHUNK]
+                    )
+                quantize(codes[:, lo:hi], y_scales[:, g, M * i + lo : M * i + hi], y_bf16[:, 0 : PACK * (hi - lo)])
+                nc.sync.dma_start(
+                    out=out_1[g, :, M * i + lo : M * i + hi, :].rearrange("p m t -> p (m t)").bitcast(I32),
+                    in_=codes[:, lo:hi].bitcast(I32),
+                )
 
-        def run(slots):
-            for k in range(-1, len(slots)):
-                if k >= 0:
-                    for pe, main in slots[k]:
-                        main()
-                if k + 1 < len(slots):
-                    for pe, main in slots[k + 1]:
-                        pe()
+        turn("a", 0, 0, [0])
+        turn("a", 0, 0, [1])
+        project_on_vector(0, 0)
+        turn_b(0)
+        turn("a", 0, 1, [0, 1])
+        rows(0, 0, 0)
+        turn("a", 1, 0, [0, 1])
+        rows(0, 0, 1)
+        project_on_vector(0, 1)
+        turn("a", 1, 1, [0, 1])
+        project_beside_vector(1, 0)
+        columns(0)
+        project_beside_vector(1, 1)
+        turn_b(1)
+        logits(0)
+        rows(0, 1, 0)
+        rows(0, 1, 1)
+        terms(0, 0, STATS)
+        logits(1)
 
-        TURNED = []
-        QE = "PPGG"
-        def keys(i):
-            return [("a", i, 0, 0), ("a", i, 0, 1), ("a", i, 1, 0), ("a", i, 1, 1), ("b", i, 0), ("b", i, 1), ("b", i, 2)]
+        columns(1)
+        spread(0)
+        results(0, 0)
+        rows(1, 0, 0)
+        rows(1, 0, 1)
+        results(0, 1)
+        terms(1, 0, M_TILES + PACK)
+        rows(1, 1, 0)
+        rows(1, 1, 1)
+        spread(1)
+        terms(1, M_TILES + PACK, STATS)
 
-        def item(unit, n, needs, gives):
-            return (both(unit[0], unit[1]) if n == 1 else unit[n], needs, gives)
+        planes(0, 0, [pack_on_gpsimd] * 3, M_PARTS)
+        planes(0, 1, [pack_on_vector] * 3, M_PARTS)
+        results(1, 0)
+        results(1, 1)
+        shared = [pack_on_scalar, pack_on_vector, pack_on_vector]
+        planes(1, 0, shared, M_PARTS)
+        planes(1, 1, shared, [(c, c + CHUNK) for c in range(0, M, CHUNK)])
 
-        def T(k):
-            return item(turn(k), 1, [], [("T", k)])
-
-        def TQ(k):
-            return item(turn(k), 2, [("T", k)], [("TQ", k)])
-
-        def PV(i, g, s):
-            return item(project_tile(i, g, s), 1, [("TQ", ("a", i, g, s // 2))], [])
-
-        def PS(i, g, t):
-            return item(project_slot(i, g, t), 1, [("TQ", ("a", i, g, 0)), ("TQ", ("a", i, g, 1))], [("PS", i, g, t)])
-
-        def IL(i, g, h, eng):
-            return (interleave_q(i, g, h, eng), [("PS", i, g, 3)], [("IL", i, g, h)])
-
-        def QQ(i, g, h, needs=()):
-            return (quant_q(i, g, h), list(needs), [("QQ", i, g, h)])
-
-        def A(i, g, h):
-            parts = row_pair(i, g, h)
-            return [(parts[n], [], [("A", i, g, h)] if n == 3 else []) for n in range(4)]
-
-        def BB(i, g, t):
-            return (row_pair(i, g, t // 2)[4 + t % 2], [("A", i, g, t // 2)], [("B", i, g, t)])
-
-        def CC(i, j, g):
-            return item(column_half(i, j, g), 1, [], [("C", i, j, g)])
-
-        def DD(i, j):
-            return item(column_half(i, j, 1), 2, [("C", i, j, 1)], [("D", i, j)])
-
-        def cols(i):
-            out = [CC(i, 0, 0)]
-            for j in range(5):
-                out += [CC(i, j + 1, 0), CC(i, j, 1)]
-            return out + [CC(i, 5, 1)]
-
-        def EV(i, g, t, ev):
-            return item(result_tile(i, g, t), 1, [("cb", i), ("term", ev), ("B", i, g, t)], [("E", i, g, t)])
-
-        def ES(i, g, t, ev):
-            return item(result_turned(i, g, t), 1, [("nterm", i), ("term", ev), ("B", i, g, t)], [("E", i, g, t)])
-
-        def F(i, g, k, eng):
-            return item(plane_chunk(i, g, k, eng), 1, [("E", i, g, t) for t in range(4)], [("F", i, g, k)])
-
-        def FQ(i, g, k):
-            return item(plane_chunk(i, g, k, "S"), 2, [("F", i, g, k)], [])
-
-        def SP(i):
-            return (spread(i), [("nterm", i)], [("cb", i)])
-
-        def Z(ks):
-            return [(logits(k, e), [("T", k)], [("Z", k, e)]) for k in ks for e in range(2)]
-
-        def match(i, ks):
-            pick, fold, size, low, decay = matchability(i)
-            return ([(pick, [("Z", k, 1) for k in ks], []), (fold, [], [("fold", i)]), (low, [("size", i)], [])],
-                    [(size, [("fold", i)], [("size", i)]), (decay, [], [("ez", i)])])
-
-        def chain(i, lo, hi, ev, needs):
-            steps, exps = terms(i, lo, hi)
-            need = {0: needs + [("ez", i)], 3: [("e0", ev)], 8: [("e1", ev)]}
-            give = {1: [("g0", ev)], 6: [("g1", ev)], 13: [("term", ev)], 14: [("nterm", i)]}
-            return ([(f, need.get(n, []), give.get(n, [])) for n, f in enumerate(steps)],
-                    [(exps[0], [("g0", ev)], [("e0", ev)]), (exps[1], [("g1", ev)], [("e1", ev)])])
-
-        def chain_ln(i, lo, hi, ev, needs):
-            first, ln, end = terms_ln(i, lo, hi)
-            v = [(first, needs + [("ez", i)], [("g0", ev)]), (end, [("e0", ev)], [("term", ev)]), (terms(i, lo, hi)[0][14] if TURNED else nothing, [], [("nterm", i)])]
-            return v, [(ln, [("g0", ev)], [("e0", ev)]), (nothing, [], [])]
-
-        def weave(big, small, start=0, per=1):
-            out = []
-            for n, it in enumerate(big):
-                out.append(it)
-                if n >= start:
-                    out += small[(n - start) * per : (n - start + 1) * per]
-            return out + small[max(0, len(big) - start) * per :]
-
-        def run_lanes(lanes):
-            done = set()
-            at = [0] * len(lanes)
-            for turn_no in range(sum(len(lane) for lane in lanes)):
-                for n, lane in enumerate(lanes):
-                    if at[n] < len(lane) and all(need in done for need in lane[at[n]][1]):
-                        lane[at[n]][0]()
-                        done.update(lane[at[n]][2])
-                        at[n] += 1
-            assert at == [len(lane) for lane in lanes], at
-
-        k0, k1 = keys(0), keys(1)
-        def after(items, need):
-            return [(items[0][0], items[0][1] + [need], items[0][2])] + items[1:]
-
-        def EVs(i, g, ev):
-            return [EV(i, g, t, ev) for t in range(4) if t % 2 or (i, g, t // 2) not in TURNED]
-
-        def ESs(i, g, ev):
-            return [ES(i, g, t, ev) for t in range(4) if t % 2 == 0 and (i, g, t // 2) in TURNED]
-
-        m0v, m0s = match(0, k0)
-        m1v, m1s = match(1, k1)
-        c0v, c0s = chain(0, 0, STATS, 0, [("D", 0, 5), ("B", 0, 1, 3)])
-        c1v, c1s = chain_ln(1, 0, 10, 1, [("D", 1, 5), ("B", 1, 0, 3)])
-        last = terms_ln(1, 10, STATS)
-        FE = "SSSSSSSSVSVV"
-        fs = [F(n // 6, n // 3 % 2, n % 3, FE[n]) for n in range(12)]
-
-        def on(eng, lo, hi):
-            return [fs[n] for n in range(lo, hi) if FE[n] == eng]
-
-        def FQs(i, g):
-            n = 6 * i + 3 * g
-            return [FQ(i, g, k) for k in range(3) if FE[n + k] == "V"] + [FQ(i, g, k) for k in range(3) if FE[n + k] != "V"]
-
-        def qv(i, g):
-            if QE[2 * i + g] == "P":
-                return [PV(i, g, 0), PV(i, g, 1), PV(i, g, 2), QQ(i, g, 0), PV(i, g, 3), QQ(i, g, 1)]
-            return [QQ(i, g, h, [("IL", i, g, h)]) for h in range(2)]
-
-        def qs(i, g):
-            return [] if QE[2 * i + g] == "P" else [PS(i, g, t) for t in range(4)]
-
-        def qg(i, g):
-            return [] if QE[2 * i + g] == "P" else [IL(i, g, h, "G") for h in range(2)]
-
-        vector = [TQ(k0[0]), PV(0, 0, 0), TQ(k0[1]), PV(0, 0, 1), TQ(k0[4]), PV(0, 0, 2), QQ(0, 0, 0), TQ(k0[5]), PV(0, 0, 3), TQ(k0[6]),
-                  QQ(0, 0, 1)] + A(0, 0, 0) + [TQ(k0[2]), TQ(k0[3])] + A(0, 0, 1)
-        vector += weave(qv(0, 1), [TQ(k) for k in k1[0:4]]) + cols(0) + A(0, 1, 0) + [m0v[0]] + A(0, 1, 1)[0:2] + [m0v[1]] + A(0, 1, 1)[2:]
-        vector += weave(qv(1, 0) + qv(1, 1), [TQ(k) for k in k1[4:]])
-        vector += weave(cols(1) + A(1, 0, 0), [m0v[2]] + c0v, 0, 1) + [SP(0), m1v[0]]
-        vector += EVs(0, 0, 0) + [m1v[1]] + EVs(0, 1, 0) + A(1, 0, 1) + [m1v[2]] + A(1, 1, 0)[0:2]
-        vector += weave(A(1, 1, 0)[2:] + A(1, 1, 1) + on("V", 0, 6) + FQs(0, 0) + FQs(0, 1), c1v, 0, 1)
-        e10, e11 = EVs(1, 0, 1), EVs(1, 1, 2)
-        vector += [SP(1), (last[0], [("B", 1, 1, 3)], [("lx",)])] + e10 + [(last[2], [("ln",)], [("term", 2)])] + on("V", 6, 9) + e11 + FQs(1, 0) + on("V", 9, 12) + FQs(1, 1)
-        scalar = [T(k0[n]) for n in (0, 1, 4, 5, 6, 2, 3)] + qs(0, 1) + [T(k1[0]), BB(0, 0, 0), T(k1[1]), BB(0, 0, 1), T(k1[2]), T(k1[3])]
-        scalar += [BB(0, 0, 2), BB(0, 0, 3)] + weave([DD(0, j) for j in range(6)], qs(1, 0) + qs(1, 1) + [T(k) for k in k1[4:]], 0, 2)
-        scalar += [BB(0, 1, 0), BB(0, 1, 1), BB(0, 1, 2), BB(0, 1, 3), m0s[0], m0s[1], DD(1, 0), c0s[0], DD(1, 1), DD(1, 2), c0s[1], DD(1, 3), DD(1, 4), DD(1, 5)]
-        s0 = on("S", 0, 6)
-        scalar += [BB(1, 0, 0), BB(1, 0, 1)] + ESs(0, 0, 0) + ESs(0, 1, 0) + s0[0:1] + [m1s[0]] + s0[1:2] + [m1s[1]] + s0[2:3] + [BB(1, 0, 2), BB(1, 0, 3)]
-        scalar += [BB(1, 1, 0), c1s[0], BB(1, 1, 1)] + s0[3:4] + [c1s[1], BB(1, 1, 2), BB(1, 1, 3)] + s0[4:]
-        scalar += [(last[1], [("lx",)], [("ln",)])] + ESs(1, 0, 1) + ESs(1, 1, 2) + on("S", 6, 12)
-        others = qg(0, 1) + after(Z(k0), ("C", 0, 0, 0)) + qg(1, 0) + qg(1, 1) + after(Z(k1), ("C", 1, 0, 0)) + on("G", 0, 12)
-        run_lanes([vector, scalar, others])
-        for quad in range(4):
+        for quad in range(QUADS):
             nc.sync.dma_start(
                 out=out_2[:, 4 * quad : 4 * quad + 4, :].rearrange("g r m -> r g m").bitcast(I32),
                 in_=y_scales[32 * quad : 32 * quad + 4, :, :].bitcast(I32),

import math
from contextlib import ExitStack

import concourse.mybir as mybir
from concourse.masks import make_identity

B, N, M, D = 2, 1024, 768, 512
FLOPS = 2 * B * N * D * D + 2 * B * N * M * D

F32 = mybir.dt.float32
BF16 = mybir.dt.bfloat16
U32 = mybir.dt.uint32
I32 = mybir.dt.int32
U8 = mybir.dt.uint8
FP8X4 = mybir.dt.float8_e4m3fn_x4
FP4X4 = mybir.dt.float4_e2m1fn_x4
ALU = mybir.AluOpType
ACT = mybir.ActivationFunctionType
AXIS = mybir.AxisListType

P = 128
PACK = 4
BANK = 512
QUADS = 4
GROUPS = N // BANK
M_TILES = M // P
XB_PAIRS = M_TILES // 2
STATS = M_TILES + GROUPS * PACK
M_PARTS = ((0, BANK), (BANK, M))
CHUNK = 256
SCALE = 1.0 / math.sqrt(D)
HALF_CONST = 0.5 * (math.log(N) + math.log(M))
GATHER_PAD = P - 32
RAW_BUFS = 10


def tile_lightgluematchabilityassignment_x2_kernel(
    tc, xa, xb, w_words, w_scales, b, wza, wzb, out_0, out_1, out_2
):
    nc = tc.nc
    with ExitStack() as ctx:
        keep = ctx.enter_context(tc.tile_pool(name="keep", bufs=1))
        rot = ctx.enter_context(tc.tile_pool(name="rot", bufs=2))
        psum_v = ctx.enter_context(tc.psum_pool(name="psum_v", bufs=4))
        psum_s = ctx.enter_context(tc.psum_pool(name="psum_s", bufs=3))
        psum_z = ctx.enter_context(tc.psum_pool(name="psum_z", bufs=1))

        def kept(name, shape, dtype):
            return keep.tile(shape, dtype, name=name, align_bytes=64)

        def bank_v():
            return psum_v.tile([P, BANK], F32, name="bank_v")

        def bank_s():
            return psum_s.tile([P, BANK], F32, name="bank_s")

        w_raw = kept("w_raw", [P, 2 * D], U8)
        ws_raw = kept("ws_raw", [P, D], U8)
        w_codes = kept("w_codes", [P, 2 * D], U8)
        w_sc = kept("w_sc", [P, D], U8)
        ident = kept("ident", [P, P], F32)
        gather = kept("gather", [P, GATHER_PAD + P], F32)
        own_slot = kept("own_slot", [P, PACK], F32)
        b_sb = kept("b_sb", [P, PACK], BF16)
        wza_sb = kept("wza_sb", [P, PACK], BF16)
        wzb_sb = kept("wzb_sb", [P, PACK], BF16)
        preload_in = kept("preload_in", [P, 1], F32)
        preload_out = kept("preload_out", [P, 1], F32)
        y_scales = kept("y_scales", [P, GROUPS, B * M], U8)
        z_bank = psum_z.tile([P, BANK], F32, name="z_bank")

        nc.vector.memset(ws_raw[:].bitcast(I32), 0)
        nc.vector.memset(preload_in[:], 0.0)
        nc.scalar.activation(out=preload_out[:], in_=preload_in[:], func=ACT.Exp)

        with tc.manual_schedule(engines={mybir.EngineType.Pool}):
            make_identity(nc, ident[:])
            nc.gpsimd.dma_start(out=b_sb[:], in_=b.rearrange("(p t) -> p t", t=PACK))
            nc.gpsimd.memset(gather[:], 1.0)
            nc.gpsimd.affine_select(
                out=gather[:], in_=gather[:], compare_op=ALU.is_ge, fill=0.0,
                base=PACK * GATHER_PAD, pattern=[[-PACK, GATHER_PAD + P]], channel_multiplier=1,
            )
            nc.gpsimd.affine_select(
                out=gather[:], in_=gather[:], compare_op=ALU.is_ge, fill=0.0,
                base=PACK - 1 - PACK * GATHER_PAD, pattern=[[PACK, GATHER_PAD + P]], channel_multiplier=-1,
            )
            nc.gpsimd.dma_start(out=wza_sb[:], in_=wza.rearrange("(p t) -> p t", t=PACK))
            nc.gpsimd.dma_start(out=wzb_sb[:], in_=wzb.rearrange("(p t) -> p t", t=PACK))

        raw = {}

        def load_a(i, g, h):
            raw["a", i, g, h] = rot.tile([P, 2, D], BF16, name="raw", bufs=RAW_BUFS)
            points = xa[i, g * BANK : (g + 1) * BANK, :].rearrange("(p t) d -> p t d", t=PACK)
            nc.sync.dma_start(out=raw["a", i, g, h][:], in_=points[:, 2 * h : 2 * h + 2, :])

        def load_b(i, h):
            raw["b", i, 0, h] = rot.tile([P, 2, D], BF16, name="raw", bufs=RAW_BUFS)
            points = xb[i, 2 * P * h : 2 * P * (h + 1), :].rearrange("(j p) d -> p j d", p=P)
            nc.sync.dma_start(out=raw["b", i, 0, h][:], in_=points)

        with tc.manual_schedule(engines={mybir.EngineType.SP}):
            load_a(0, 0, 0)
            nc.sync.dma_start(out=w_raw[:].bitcast(I32), in_=w_words[0].bitcast(I32))
            load_a(0, 0, 1)
            for quad in range(QUADS):
                nc.sync.dma_start(
                    out=ws_raw[32 * quad : 32 * quad + 4, :].bitcast(I32),
                    in_=w_scales[0, 4 * quad : 4 * quad + 4, :].bitcast(I32),
                )
            for h in range(XB_PAIRS):
                load_b(0, h)
            for i, g in ((0, 1), (1, 0), (1, 1)):
                for h in range(2):
                    load_a(i, g, h)
            for h in range(XB_PAIRS):
                load_b(1, h)

        nc.vector.tensor_copy(
            out=w_codes[:].rearrange("p (t m e) -> p t m e", t=PACK, e=2),
            in_=w_raw[:].rearrange("p (m t e) -> p t m e", t=PACK, e=2),
        )
        nc.vector.tensor_copy(
            out=w_sc[:].rearrange("p (t m) -> p t m", t=PACK),
            in_=ws_raw[:].rearrange("p (m t) -> p t m", t=PACK),
        )
        nc.vector.tensor_reduce(
            out=own_slot[:], in_=ident[:].rearrange("p (a t) -> p t a", t=PACK), axis=AXIS.X, op=ALU.add
        )

        def quantize(codes, scales, grouped):
            nc.vector.quantize_mx(out=codes.bitcast(FP8X4), scales=scales, in_=grouped)

        def mx_scores(out, lhs, rhs, lhs_cols, rhs_cols):
            with tc.high_priority():
                nc.tensor.matmul_mx(
                    out=out, lhsT=lhs[0][:, lhs_cols].bitcast(FP8X4), lhsT_scale=lhs[1][:, lhs_cols],
                    rhs=rhs[0][:, rhs_cols].bitcast(FP8X4), rhs_scale=rhs[1][:, rhs_cols], start=True, stop=True,
                )

        def mx_project(out, t, rhs, rhs_cols):
            nc.tensor.matmul_mx(
                out=out, lhsT=w_codes[:, 2 * P * t : 2 * P * (t + 1)].bitcast(FP4X4),
                lhsT_scale=w_sc[:, P * t : P * (t + 1)],
                rhs=rhs[0][:, rhs_cols].bitcast(FP8X4), rhs_scale=rhs[1][:, rhs_cols], start=True, stop=True,
            )

        def operand(name, width):
            return (kept(name + "_codes", [P, width], U32), kept(name + "_scales", [P, width], U8))

        xa_mx = {(i, g): operand("xa%d%d" % (i, g), BANK) for i in range(B) for g in range(GROUPS)}
        q_mx = {(i, g): operand("q%d%d" % (i, g), BANK) for i in range(B) for g in range(GROUPS)}
        xb_mx = {i: operand("xb%d" % i, M) for i in range(B)}
        y = {(i, g): kept("y%d%d" % (i, g), [P, PACK, M], F32) for i in range(B) for g in range(GROUPS)}
        stat = {
            (name, i): kept("%s%d" % (name, i), [P, STATS], F32)
            for name in ("first", "low", "shift", "total", "absz", "ez", "mz", "x", "base", "ln", "term", "nterm")
            for i in range(B)
        }
        turned = {}
        col_scores = {}
        col_term = {}

        def on_scalar(t):
            return t % 2 == 0

        def turn(kind, i, g, pairs):
            tile = kept("turned_%s%d%d%d" % (kind, i, g, pairs[0]), [P, 2 * BANK * len(pairs)], BF16)
            for n, h in enumerate(pairs):
                words = raw[kind, i, g, h][:].rearrange("p a d -> p (a d)").bitcast(F32)
                ps = bank_s()
                for a in range(2):
                    for u in range(2):
                        k = 2 * a + u
                        nc.tensor.transpose(
                            ps[:, P * k : P * (k + 1)], words[:, D // 2 * a + u : D // 2 * (a + 1) : 2], ident[:]
                        )
                turned[kind, i, g, h] = tile[:, 2 * BANK * n : 2 * BANK * (n + 1)]
                nc.scalar.copy(
                    out=turned[kind, i, g, h].bitcast(F32).rearrange("p (a r u) -> p a r u", a=2, u=2),
                    in_=ps[:].rearrange("p (a u r) -> p a r u", a=2, u=2),
                )
            codes, scales = xa_mx[i, g] if kind == "a" else xb_mx[i]
            cols = slice(2 * P * pairs[0], 2 * P * (pairs[-1] + 1))
            quantize(codes[:, cols], scales[:, cols], tile[:])

        def turn_b(i):
            turn("b", i, 0, [0, 1])
            turn("b", i, 0, [2])

        def project_on_vector(i, g):
            for h in range(2):
                q_pair = rot.tile([P, 2 * P, PACK], BF16, name="q_pair", align_bytes=64)
                for a in range(2):
                    ps = bank_v()
                    points = slice(P * (2 * h + a), P * (2 * h + a + 1))
                    with tc.high_priority():
                        for t in range(PACK):
                            mx_project(ps[:, P * t : P * (t + 1)], t, xa_mx[i, g], points)
                    nc.vector.tensor_tensor(
                        out=q_pair[:, P * a : P * (a + 1), :], in0=ps[:].rearrange("p (t n) -> p n t", t=PACK),
                        in1=b_sb[:].unsqueeze(1).to_broadcast([P, P, PACK]), op=ALU.add,
                    )
                cols = slice(2 * P * h, 2 * P * (h + 1))
                quantize(q_mx[i, g][0][:, cols], q_mx[i, g][1][:, cols], q_pair[:].rearrange("p n t -> p (n t)"))

        def project_beside_vector(i, g):
            q_slices = rot.tile([P, PACK, BANK], BF16, name="q_slices", align_bytes=64)
            for t in range(PACK):
                ps = bank_s()
                mx_project(ps[:], t, xa_mx[i, g], slice(0, BANK))
                nc.scalar.activation(out=q_slices[:, t, :], in_=ps[:], func=ACT.Identity, bias=b_sb[:, t : t + 1])
            q_group = rot.tile([P, BANK, PACK], BF16, name="q_group", align_bytes=64)
            for h in range(2):
                cols = slice(2 * P * h, 2 * P * (h + 1))
                nc.gpsimd.tensor_scalar(
                    out=q_group[:, cols, :], in0=q_slices[:, :, cols].rearrange("p t n -> p n t"),
                    scalar1=1.0, scalar2=0.0, op0=ALU.mult, op1=ALU.add,
                )
            quantize(q_mx[i, g][0][:], q_mx[i, g][1][:], q_group[:].rearrange("p n t -> p (n t)"))

        def logits(i):
            tiles = [("b", 0, h, a, 2 * h + a) for h in range(XB_PAIRS) for a in range(2)]
            tiles += [
                ("a", g, h, a, M_TILES + PACK * g + 2 * h + a) for g in range(GROUPS) for h in range(2) for a in range(2)
            ]
            for kind, g, h, a, k in tiles:
                for q in range(QUADS):
                    col = PACK * (STATS * (QUADS * i + q) + k)
                    lo = BANK * a + P * q
                    nc.tensor.matmul(
                        z_bank[:, col : col + PACK], lhsT=turned[kind, i, g, h][:, lo : lo + P],
                        rhs=(wza_sb if kind == "a" else wzb_sb)[:], start=True, stop=True,
                    )
            n = QUADS * STATS
            picked = kept("picked%d" % i, [P, n, PACK], F32)
            folded = kept("folded%d" % i, [P, n], F32)
            z = z_bank[:, B * PACK * n + STATS * i : B * PACK * n + STATS * (i + 1)]
            nc.vector.tensor_tensor(
                out=picked[:], in0=z_bank[:, PACK * n * i : PACK * n * (i + 1)].rearrange("p (c t) -> p c t", t=PACK),
                in1=own_slot[:].unsqueeze(1).to_broadcast([P, n, PACK]), op=ALU.mult,
            )
            nc.vector.tensor_reduce(out=folded[:], in_=picked[:], axis=AXIS.X, op=ALU.add)
            for q in range(QUADS):
                nc.tensor.matmul(
                    z, lhsT=gather[:, GATHER_PAD - 32 * q : GATHER_PAD - 32 * q + P],
                    rhs=folded[:, STATS * q : STATS * (q + 1)], start=(q == 0), stop=(q == QUADS - 1),
                )
            nc.scalar.activation(out=stat["absz", i][:], in_=z, func=ACT.Abs)
            nc.vector.tensor_scalar(
                out=stat["mz", i][:], in0=z, scalar1=0.0, scalar2=HALF_CONST, op0=ALU.min, op1=ALU.add
            )
            nc.scalar.activation(out=stat["ez", i][:], in_=stat["absz", i][:], func=ACT.Exp, scale=-1.0)

        def empty_scores(src, dst, factor, first, least):
            nc.vector.tensor_scalar(
                out=dst, in0=src, scalar1=factor, scalar2=first, op0=ALU.mult, op1=ALU.min, accum_out=least
            )

        def exp_sum(i, k, src, factor):
            exps = rot.tile([P, N], BF16, name="exps", bufs=3)
            nc.scalar.activation(
                out=exps[:, 0 : src.shape[1]], in_=src, func=ACT.Exp, scale=factor,
                bias=stat["shift", i][:, k : k + 1], accum_out=stat["total", i][:, k : k + 1],
            )

        def rows(i, g, h):
            slots = (2 * h, 2 * h + 1)
            k0 = M_TILES + PACK * g
            for lo, hi in M_PARTS:
                for t in slots:
                    k = k0 + t
                    ps = bank_v()
                    mx_scores(ps[:, 0 : hi - lo], q_mx[i, g], xb_mx[i], slice(P * t, P * (t + 1)), slice(lo, hi))
                    first = stat["first", i][:, k : k + 1]
                    last = stat["shift" if on_scalar(t) else "low", i][:, k : k + 1]
                    empty_scores(
                        ps[:, 0 : hi - lo], y[i, g][:, t, lo:hi], -SCALE if on_scalar(t) else -2.0 * SCALE,
                        first if lo else None, last if lo else first,
                    )
            odd = slice(k0 + slots[1], k0 + slots[1] + 1)
            nc.scalar.activation(out=stat["shift", i][:, odd], in_=stat["low", i][:, odd], func=ACT.Copy, scale=0.5)
            for t in slots:
                exp_sum(i, k0 + t, y[i, g][:, t, :], -1.0 if on_scalar(t) else -0.5)

        def column_half(i, j, g):
            if g == 0:
                col_scores[i, j] = rot.tile([P, N], F32, name="col_scores", bufs=B * M_TILES)
            ps = bank_v()
            mx_scores(ps[:], xb_mx[i], q_mx[i, g], slice(P * j, P * (j + 1)), slice(0, BANK))
            first = stat["first", i][:, j : j + 1]
            empty_scores(
                ps[:], col_scores[i, j][:, BANK * g : BANK * (g + 1)], -SCALE,
                first if g else None, stat["shift", i][:, j : j + 1] if g else first,
            )
            if g == 1:
                exp_sum(i, j, col_scores[i, j][:], -1.0)

        def columns(i):
            column_half(i, 0, 0)
            for j in range(1, M_TILES):
                column_half(i, j, 0)
                column_half(i, j - 1, 1)
            column_half(i, M_TILES - 1, 1)

        def terms(i, lo, hi):
            s = {name: stat[name, i][:, lo:hi] for name in ("x", "ez", "total", "ln", "base", "shift", "mz", "term")}
            nc.vector.scalar_tensor_tensor(
                out=s["x"], in0=s["ez"], scalar=1.0, in1=s["total"], op0=ALU.add, op1=ALU.mult
            )
            nc.scalar.activation(out=s["ln"], in_=s["x"], func=ACT.Ln)
            nc.vector.tensor_tensor(out=s["base"], in0=s["shift"], in1=s["mz"], op=ALU.add)
            nc.vector.tensor_tensor(out=s["term"], in0=s["base"], in1=s["ln"], op=ALU.subtract)
            if lo == 0:
                nc.vector.tensor_scalar(
                    out=stat["nterm", i][:, 0:M_TILES], in0=stat["term", i][:, 0:M_TILES],
                    scalar1=-0.5, scalar2=None, op0=ALU.mult,
                )

        def spread(i):
            ps = [bank_v(), bank_v()]
            with tc.high_priority():
                for j in range(M_TILES):
                    nc.tensor.transpose(
                        ps[j // 4][:, P * (j % 4) : P * (j % 4 + 1)],
                        stat["term", i][:, j : j + 1].to_broadcast([P, P]), ident[:],
                    )
            col_term[i] = ps

        def results(i, g):
            out_rows = out_0[i, g * BANK : (g + 1) * BANK, :].rearrange("(p t) m -> p t m", t=PACK)
            for t in range(PACK):
                k = M_TILES + PACK * g + t
                row_term = stat["term", i][:, k : k + 1]
                if on_scalar(t):
                    points = slice(BANK * g + P * t, BANK * g + P * (t + 1))
                    ps = [bank_s(), bank_s()]
                    for j in range(M_TILES):
                        dst = ps[j // 4][:, P * (j % 4) : P * (j % 4 + 1)]
                        nc.tensor.matmul(
                            dst, lhsT=col_scores[i, j][:, points], rhs=ident[:],
                            is_transpose=True, start=True, stop=False,
                        )
                        nc.tensor.matmul(
                            dst, lhsT=stat["nterm", i][:, j : j + 1].to_broadcast([P, P]), rhs=ident[:],
                            is_transpose=True, start=False, stop=True,
                        )
                    for n, (lo, hi) in enumerate(M_PARTS):
                        nc.scalar.activation(
                            out=y[i, g][:, t, lo:hi], in_=ps[n][:, 0 : hi - lo], func=ACT.Identity,
                            scale=-2.0, bias=row_term,
                        )
                else:
                    for n, (lo, hi) in enumerate(M_PARTS):
                        nc.vector.scalar_tensor_tensor(
                            out=y[i, g][:, t, lo:hi], in0=col_term[i][n][:, 0 : hi - lo], scalar=row_term,
                            in1=y[i, g][:, t, lo:hi], op0=ALU.add, op1=ALU.subtract,
                        )
                nc.sync.dma_start(out=out_rows[:, t, :], in_=y[i, g][:, t, :])

        def pack_on_gpsimd(dst, src):
            nc.gpsimd.tensor_scalar(
                out=dst.rearrange("p (m t) -> p m t", t=PACK), in0=src.rearrange("p t m -> p m t"),
                scalar1=1.0, scalar2=0.0, op0=ALU.mult, op1=ALU.add,
            )

        def pack_with(copy):
            def pack(dst, src):
                copy(
                    out=dst.rearrange("p (c e t) -> p c t e", e=4, t=PACK),
                    in_=src.rearrange("p t (c e) -> p c t e", e=4),
                )

            return pack

        pack_on_scalar = pack_with(nc.scalar.copy)
        pack_on_vector = pack_with(nc.vector.tensor_copy)

        def planes(i, g, packers, parts):
            codes = rot.tile([P, M], U32, name="y_codes", align_bytes=64)
            for lo, hi in parts:
                y_bf16 = rot.tile([P, BANK * PACK], BF16, name="y_bf16", bufs=3, align_bytes=64)
                for c in range(lo, hi, CHUNK):
                    packers[c // CHUNK](
                        y_bf16[:, PACK * (c - lo) : PACK * (c - lo + CHUNK)], y[i, g][:, :, c : c + CHUNK]
                    )
                quantize(codes[:, lo:hi], y_scales[:, g, M * i + lo : M * i + hi], y_bf16[:, 0 : PACK * (hi - lo)])
                nc.sync.dma_start(
                    out=out_1[g, :, M * i + lo : M * i + hi, :].rearrange("p m t -> p (m t)").bitcast(I32),
                    in_=codes[:, lo:hi].bitcast(I32),
                )

        turn("a", 0, 0, [0])
        turn("a", 0, 0, [1])
        project_on_vector(0, 0)
        turn_b(0)
        turn("a", 0, 1, [0, 1])
        rows(0, 0, 0)
        turn("a", 1, 0, [0, 1])
        rows(0, 0, 1)
        project_on_vector(0, 1)
        turn("a", 1, 1, [0, 1])
        project_beside_vector(1, 0)
        columns(0)
        project_beside_vector(1, 1)
        turn_b(1)
        logits(0)
        rows(0, 1, 0)
        rows(0, 1, 1)
        terms(0, 0, STATS)
        logits(1)

        columns(1)
        spread(0)
        results(0, 0)
        rows(1, 0, 0)
        rows(1, 0, 1)
        results(0, 1)
        terms(1, 0, M_TILES + PACK)
        rows(1, 1, 0)
        rows(1, 1, 1)
        spread(1)
        terms(1, M_TILES + PACK, STATS)

        planes(0, 0, [pack_on_gpsimd] * 3, M_PARTS)
        planes(0, 1, [pack_on_vector] * 3, M_PARTS)
        results(1, 0)
        results(1, 1)
        shared = [pack_on_scalar, pack_on_vector, pack_on_vector]
        planes(1, 0, shared, M_PARTS)
        planes(1, 1, shared, [(c, c + CHUNK) for c in range(0, M, CHUNK)])

        for quad in range(QUADS):
            nc.sync.dma_start(
                out=out_2[:, 4 * quad : 4 * quad + 4, :].rearrange("g r m -> r g m").bitcast(I32),
                in_=y_scales[32 * quad : 32 * quad + 4, :, :].bitcast(I32),
            )
